import numpy as np
import ml_dtypes


def mxq(x, axis, fmt="e4m3"):
    dtype, down = {"e4m3": (ml_dtypes.float8_e4m3fn, 7), "e5m2": (ml_dtypes.float8_e5m2, 14)}[fmt]
    v = np.moveaxis(np.asarray(x, np.float32).astype(ml_dtypes.bfloat16).astype(np.float64), axis, -1)
    blocks = v.reshape(v.shape[:-1] + (-1, 32))
    amax = np.abs(blocks).max(-1, keepdims=True)
    byte = np.maximum(np.where(amax > 0, np.frexp(amax)[1] - 1 + 127, 0) - down, 1)
    scale = np.exp2(byte - 127.0)
    codes = (blocks / scale).astype(np.float32).astype(dtype).astype(np.float64)
    return np.moveaxis((codes * scale).reshape(v.shape), -1, axis)


WIDE = False


def mx_kscale(k):
    if not WIDE:
        return np.ones(k)
    levels = np.array([10, -10, 5, -5, 0])
    if k % 512:
        return np.exp2(np.random.permutation(np.resize(levels, k // 32))).repeat(32)
    a = np.empty((k // 512, 16))
    for p in range(k // 512):
        a[p, :8] = np.random.permutation(np.resize(levels, 8))
        for g in range(8):
            far = levels[np.abs(levels - a[p, g]) >= 10]
            a[p, g + 8] = far[np.random.randint(len(far))]
    return np.exp2(a.ravel()).repeat(32)


def f64(x):
    return np.asarray(x).astype(np.float64)


def striped(idx):
    return np.tile(idx.reshape(-1, 16).T, (8, 1)).astype(np.uint16)


def unstriped(offs):
    return offs[:16].T.reshape(-1).astype(np.int64)


E2M1 = np.array([0.0, 0.5, 1.0, 1.5, 2.0, 3.0, 4.0, 6.0, -0.0, -0.5, -1.0, -1.5, -2.0, -3.0, -4.0, -6.0])


def pack_weight(w, fmt):
    k, n = w.shape
    w = f64(np.asarray(w, np.float32).astype(ml_dtypes.bfloat16)).reshape(k // 32, 32, n)
    amax = np.abs(w).max(1)
    if fmt == "e4m3":
        byte = np.frexp(amax)[1] - 1 + 127 - 7
    else:
        mant, ex = np.frexp(amax / 6.0)
        byte = np.where(mant > 0.5, ex, ex - 1) + 127
    byte = np.clip(np.where(amax > 0, byte, 1), 1, 254)
    scaled = (w * np.exp2(127.0 - byte)[:, None, :]).reshape(k, n).astype(np.float32)
    by_word = np.ascontiguousarray(scaled.reshape(k // 512, 128, 4, n).transpose(0, 1, 3, 2))
    if fmt == "e4m3":
        words = by_word.astype(ml_dtypes.float8_e4m3fn).view(np.uint8)
    else:
        c = by_word.astype(ml_dtypes.float4_e2m1fn).view(np.uint8) & 0xF
        words = (c[..., 0::2] | (c[..., 1::2] << 4)).reshape(k // 512, 128, 2 * n)
    return np.ascontiguousarray(words), np.ascontiguousarray(byte.astype(np.uint8).reshape(k // 512, 16, n))


def unpack_weight(words, scales, fmt):
    g, _, n = scales.shape
    words = np.ascontiguousarray(words).reshape(g, 128, n, -1)
    if fmt == "e4m3":
        vals = words.view(ml_dtypes.float8_e4m3fn).astype(np.float64)
    else:
        nib = np.empty((g, 128, n, 4), np.uint8)
        nib[..., 0::2] = words & 0xF
        nib[..., 1::2] = words >> 4
        vals = E2M1[nib]
    vals = vals * np.repeat(np.exp2(scales.astype(np.float64) - 127.0), 8, axis=1)[..., None]
    return vals.transpose(0, 1, 3, 2).reshape(g * 512, n)


def gelu(v):
    return 0.5 * v * (1.0 + np.tanh(np.sqrt(2.0 / np.pi) * (v + 0.044715 * v**3)))


def pack_table4(v):
    words, scales = pack_weight(v, "e2m1")
    g, t = words.shape[0] // 2, v.shape[1]
    words = words.reshape(g, 2, 128, t, 2).transpose(0, 2, 3, 1, 4)
    return np.concatenate([words.reshape(g, -1), scales.reshape(g, -1)], axis=1)


def unpack_table4(tab):
    g, t = tab.shape[0], tab.shape[1] // 544
    words = tab[:, :512 * t].reshape(g, 128, t, 2, 2).transpose(0, 3, 1, 2, 4).reshape(2 * g, 128, 2 * t)
    return unpack_weight(words, tab[:, 512 * t:].reshape(2 * g, 16, t), "e2m1")


K, T, S, H, N = 1024, 2048, 1024, 1024, 256

def setup_inputs():
    n = np.random.standard_normal
    s = mx_kscale(K)[:, None]
    u = mx_kscale(H)[:, None]
    wb_words, wb_scales = pack_weight(n((K, H)) / np.sqrt(K) / s * u.T, "e2m1")
    wc_words, wc_scales = pack_weight(n((H, N)) / np.sqrt(H) / u, "e4m3")
    return {
        "tab": pack_table4(n((K, T)) * s),
        "offs": striped(np.random.permutation(T)[:S]),
        "wa": (n((K, H)) / np.sqrt(K) / s * u.T).astype(np.float32),
        "ba": (0.5 * n(H) * u[:, 0]).astype(np.float32),
        "wb_words": wb_words,
        "wb_scales": wb_scales,
        "bb": (0.5 * n(H) * u[:, 0]).astype(np.float32),
        "wc_words": wc_words,
        "wc_scales": wc_scales,
        "bc": (0.5 * n(N)).astype(np.float32),
    }

def reference(tab, offs, wa, ba, wb_words, wb_scales, bb, wc_words, wc_scales, bc):
    v = unpack_table4(tab)[:, unstriped(offs)]
    waq = mxq(f64(wa), 0, "e4m3")
    wbq = unpack_weight(wb_words, wb_scales, "e2m1")
    wcq = unpack_weight(wc_words, wc_scales, "e4m3")
    a = (waq.T @ v) + f64(ba)[:, None]
    b = (wbq.T @ v) + f64(bb)[:, None]
    h = np.maximum(a, b)
    hq = mxq(h, 0, "e4m3")
    return (wcq.T @ hq) + f64(bc)[:, None]

@@ -1,0 +1,279 @@
+from contextlib import ExitStack
+
+import concourse.mybir as mybir
+
+K, T, S, H, N = 1024, 2048, 1024, 1024, 256
+FLOPS = 2 * S * (2 * K * H + H * N)
+
+F32 = mybir.dt.float32
+BF16 = mybir.dt.bfloat16
+I32 = mybir.dt.int32
+U32 = mybir.dt.uint32
+U16 = mybir.dt.uint16
+U8 = mybir.dt.uint8
+FP8X4 = mybir.dt.float8_e4m3fn_x4
+FP4X4 = mybir.dt.float4_e2m1fn_x4
+IDENTITY = mybir.ActivationFunctionType.Identity
+ADD = mybir.AluOpType.add
+MAX = mybir.AluOpType.max
+
+P = 128
+PACK = 4
+PASS = P * PACK
+QUADS = 4
+QROWS = 4
+HALF = 512
+ROWS = 32
+
+
+def tile_list_stroke_maxout_logits_kernel(tc, tab, offs, wa, ba, wb_words, wb_scales, bb, wc_words, wc_scales, bc, out):
+    nc = tc.nc
+    with ExitStack() as ctx:
+        lists = ctx.enter_context(tc.tile_pool(name="lists", bufs=1))
+        keep = ctx.enter_context(tc.tile_pool(name="keep", bufs=1))
+        psum = ctx.enter_context(tc.psum_pool(name="psum", bufs=1))
+
+        def held(name, shape, dtype, tag=""):
+            return keep.tile(shape, dtype, name=name, tag=tag or name, align_bytes=64)
+
+        offsets = lists.tile([P, S // 16], U16, name="offsets")
+        tab_scales = held("tab_scales", [P, T // 4], I32)
+        tab_words = held("tab_words", [P, T], I32)
+        wb_scales_raw = held("wb_scales_raw", [P, H // 4], I32)
+        wb_raw = [held("wb_raw_%d" % g, [P, 2, PASS // 2], I32) for g in range(2)]
+        wb_planes = held("wb_planes", [P, 2, H // 4], I32)
+        ba_sb = held("ba_sb", [P, 2, PACK], F32)
+        bb_sb = held("bb_sb", [P, 2, PACK], F32)
+        bc_sb = held("bc_sb", [P, 2], F32)
+        v_planes = [held("v_planes_%d" % u, [P, 2, HALF // 4], I32) for u in range(2)]
+        wa_raw = {}
+
+        def load_wa(g, a, tag, pieces=1):
+            wa_raw[g, a] = held("wa_raw_%d_%d" % (g, a), [P, PACK, PASS], F32, tag)
+            rows = wa[PASS * a : PASS * (a + 1), PASS * g : PASS * (g + 1)].rearrange("(p j) c -> p j c", j=PACK)
+            for i in range(pieces):
+                cols = slice(i * PASS // pieces, (i + 1) * PASS // pieces)
+                nc.sync.dma_start(out=wa_raw[g, a][:, :, cols], in_=rows[:, :, cols])
+
+        def spread_planes(queue, planes, rows):
+            for q in range(QUADS):
+                queue.dma_start(out=planes[32 * q : 32 * q + QROWS, :, :], in_=rows[2 * QROWS * q : 2 * QROWS * (q + 1), :].bitcast(I32))
+
+        nc.sync.dma_start(offsets[:], offs)
+        nc.sync.dma_start(out=tab_scales[:ROWS, :], in_=tab[0, 512 * T :].rearrange("(a q t) -> q a t", a=2, q=16).bitcast(I32))
+        nc.sync.dma_start(out=wb_scales_raw[:ROWS, :], in_=wb_scales.bitcast(I32).rearrange("a q c -> q a c"))
+        nc.sync.dma_start(out=tab_words[:], in_=tab[0, : 512 * T].rearrange("(p b) -> p b", p=P).bitcast(I32))
+        for g in range(2):
+            cols = slice(g * PASS // 2, (g + 1) * PASS // 2)
+            nc.sync.dma_start(out=wb_raw[g][:], in_=wb_words.bitcast(I32)[:, :, cols].rearrange("a p c -> p a c"))
+
+        for rows in (wb_scales_raw, tab_scales):
+            nc.vector.memset(rows[ROWS : 2 * ROWS, :], 0)
+            nc.vector.memset(rows[2 * ROWS :, :], 0)
+        nc.vector.memset(wb_planes[:], 0)
+        for u in range(2):
+            nc.vector.memset(v_planes[u][:], 0)
+        nc.gpsimd.dma_start(out=bb_sb[:], in_=bb.rearrange("(g p t) -> p g t", g=2, t=PACK))
+        nc.gpsimd.dma_start(out=ba_sb[:], in_=ba.rearrange("(g p t) -> p g t", g=2, t=PACK))
+        with nc.allow_non_contiguous_dma(reason="one bias value for each partition"):
+            nc.gpsimd.dma_start(out=bc_sb[:], in_=bc.rearrange("(c p) -> p c", p=P))
+
+        wb_scale_rows = held("wb_scale_rows", [P, H], U8)
+        nc.vector.tensor_copy(
+            out=wb_scale_rows[:].rearrange("p (g t m) -> p g t m", g=2, t=PACK),
+            in_=wb_scales_raw[:].bitcast(U8).rearrange("p (g m t) -> p g t m", g=2, t=PACK),
+        )
+        spread_planes(nc.sync, wb_planes, wb_scale_rows)
+        load_wa(0, 0, "wb_scales_raw", pieces=2)
+
+        v_codes = {}
+
+        def gather_scales(u):
+            picked = held("picked_scales_%d" % u, [P, HALF], U8)
+            cols = offsets[:, u * (HALF // 16) : (u + 1) * (HALF // 16)]
+            nc.vector.tensor_copy(out=picked[:], in_=tab_scales[:].bitcast(U8).indirect(cols))
+            spread_planes(nc.scalar, v_planes[u], picked)
+
+        def gather_words(u):
+            picked = held("picked_%d" % u, [P, HALF], U32)
+            cols = offsets[:, u * (HALF // 16) : (u + 1) * (HALF // 16)]
+            nc.vector.tensor_copy(out=picked[:], in_=tab_words[:].bitcast(U32).indirect(cols))
+            parted = held("v_codes_%d" % u, [P, 2, 2 * HALF], U8)
+            nc.vector.tensor_copy(out=parted[:].bitcast(U16), in_=picked[:].bitcast(U16).rearrange("p (j a) -> p a j", a=2))
+            v_codes[u] = parted
+
+        def v_operand(u, a):
+            return v_codes[u][:, a, :].bitcast(FP4X4), v_planes[u][:, a, :].bitcast(U8)
+
+        wb_codes = {}
+
+        def permute_wb(g):
+            wb_codes[g] = held("wb_codes_%d" % g, [P, 2, 2 * PASS], U8)
+            nc.vector.tensor_copy(
+                out=wb_codes[g][:].bitcast(U16).rearrange("p a (t m) -> p a t m", t=PACK),
+                in_=wb_raw[g][:].bitcast(U16).rearrange("p a (m t) -> p a t m", t=PACK),
+            )
+
+        pairs = [(i, j) for i in range(2) for j in range(2)]
+        wa_bf16 = {key: held("wa_bf16_%d_%d" % key, [P, PACK, P, PACK], BF16) for key in pairs}
+        wa_codes = {key: held("wa_codes_%d_%d" % key, [P, PASS], U32) for key in pairs}
+        wa_planes = {key: held("wa_planes_%d_%d" % key, [P, PASS], U8) for key in pairs}
+
+        def round_wa(g, a, part, on_scalar):
+            m = slice(part * (P // 2), (part + 1) * (P // 2))
+            src = wa_raw[g, a][:].rearrange("p j (m t) -> p m j t", t=PACK)[:, m]
+            dst = wa_bf16[g, a][:].rearrange("p t m j -> p m j t")[:, m]
+            if on_scalar:
+                nc.scalar.activation(out=dst, in_=src, func=IDENTITY)
+            else:
+                nc.vector.tensor_copy(out=dst, in_=src)
+
+        def quantize_wa(g, a):
+            nc.vector.quantize_mx(
+                out=wa_codes[g, a][:].bitcast(FP8X4),
+                scales=wa_planes[g, a][:],
+                in_=wa_bf16[g, a][:].rearrange("p t m j -> p (t m j)"),
+            )
+
+        b_sums = {}
+
+        def piece_b(g, u):
+            sums = held("b_sums_%d_%d" % (g, u), [P, PACK, HALF], F32)
+            for t in range(PACK):
+                bank = psum.tile([P, HALF], F32, name="scalar_bank", bufs=4)
+                for a in range(2):
+                    codes, plane = v_operand(u, a)
+                    nc.tensor.matmul_mx(
+                        out=bank[:],
+                        lhsT=wb_codes[g][:, a, 2 * P * t : 2 * P * (t + 1)].bitcast(FP4X4),
+                        lhsT_scale=wb_planes[:].bitcast(U8)[:, a, PASS * g + P * t : PASS * g + P * (t + 1)],
+                        rhs=codes,
+                        rhs_scale=plane,
+                        start=(a == 0),
+                        stop=(a == 1),
+                    )
+                nc.scalar.activation(out=sums[:, t, :], in_=bank[:], func=IDENTITY, bias=bb_sb[:, g, t : t + 1])
+            b_sums[g, u] = sums
+
+        h_rows = {(g, u): held("h_rows_%d_%d" % (g, u), [P, PACK, HALF], BF16) for g in range(2) for u in range(2)}
+        h_grouped = {key: held("h_grouped_%d_%d" % key, [P, HALF, PACK], BF16) for key in h_rows}
+        h_codes = {key: held("h_codes_%d_%d" % key, [P, HALF], U32) for key in h_rows}
+        h_planes = {key: held("h_planes_%d_%d" % key, [P, HALF], U8) for key in h_rows}
+
+        def matmul_a(g, u, t):
+            bank = psum.tile([P, HALF], F32, name="a_bank", bufs=4)
+            for a in range(2):
+                codes, plane = v_operand(u, a)
+                nc.tensor.matmul_mx(
+                    out=bank[:],
+                    lhsT=wa_codes[g, a][:, P * t : P * (t + 1)].bitcast(FP8X4),
+                    lhsT_scale=wa_planes[g, a][:, P * t : P * (t + 1)],
+                    rhs=codes,
+                    rhs_scale=plane,
+                    start=(a == 0),
+                    stop=(a == 1),
+                )
+            return bank
+
+        def maxout(g, u, t, bank, cols):
+            nc.vector.scalar_tensor_tensor(
+                out=h_rows[g, u][:, t, cols],
+                in0=bank[:, cols],
+                scalar=ba_sb[:, g, t : t + 1],
+                in1=b_sums[g, u][:, t, cols],
+                op0=ADD,
+                op1=MAX,
+            )
+
+        def piece_a(g, u):
+            for t in range(PACK):
+                maxout(g, u, t, matmul_a(g, u, t), slice(0, HALF))
+
+        def group_h(g, u, cols, on_scalar):
+            src = h_rows[g, u][:, :, cols].rearrange("p t (c i) -> p c t i", i=4)
+            dst = h_grouped[g, u][:, cols, :].rearrange("p (c i) t -> p c t i", i=4)
+            if on_scalar:
+                nc.scalar.copy(out=dst, in_=src)
+            else:
+                nc.vector.tensor_copy(out=dst, in_=src)
+
+        def quantize_h(g, u, cols):
+            nc.vector.quantize_mx(
+                out=h_codes[g, u][:, cols].bitcast(FP8X4),
+                scales=h_planes[g, u][:, cols],
+                in_=h_grouped[g, u][:, cols, :].rearrange("p j t -> p (j t)"),
+            )
+
+        def logits(u, cols, both_engines):
+            width = cols.stop - cols.start
+            for c in range(N // P):
+                bank = psum.tile([P, HALF], F32, name="scalar_bank", bufs=4)
+                for g in range(2):
+                    nc.tensor.matmul_mx(
+                        out=bank[:, :width],
+                        lhsT=wc_codes[:, g, P * c : P * (c + 1)].bitcast(FP8X4),
+                        lhsT_scale=wc_planes[:].bitcast(U8)[QROWS * g :, P * c : P * (c + 1)],
+                        rhs=h_codes[g, u][:, cols].bitcast(FP8X4),
+                        rhs_scale=h_planes[g, u][:, cols],
+                        start=(g == 0),
+                        stop=(g == 1),
+                    )
+                result = held("result_%d_%d_%d" % (u, cols.start, c), [P, width], F32)
+                if both_engines and c == 1:
+                    nc.vector.tensor_scalar_add(out=result[:], in0=bank[:, :width], scalar1=bc_sb[:, c : c + 1])
+                else:
+                    nc.scalar.activation(out=result[:], in_=bank[:, :width], func=IDENTITY, bias=bc_sb[:, c : c + 1])
+                nc.sync.dma_start(out=out[P * c : P * (c + 1), HALF * u + cols.start : HALF * u + cols.stop], in_=result[:])
+
+        whole = slice(0, HALF)
+        chunks = [slice(0, HALF // 2), slice(HALF // 2, HALF)]
+        gather_scales(0)
+        gather_words(0)
+        permute_wb(0)
+        load_wa(0, 1, "wb_raw_0")
+        permute_wb(1)
+        round_wa(0, 0, 0, True)
+        round_wa(0, 0, 1, True)
+        piece_b(0, 0)
+        round_wa(0, 1, 0, False)
+        round_wa(0, 1, 1, False)
+        quantize_wa(0, 0)
+        quantize_wa(0, 1)
+        piece_b(1, 0)
+        load_wa(1, 0, "wb_raw_1")
+        gather_scales(1)
+        load_wa(1, 1, "tab_scales")
+        gather_words(1)
+        wc_codes = held("wc_codes", [P, 2, N], I32, "tab_words")
+        wc_planes = held("wc_planes", [P, N // 4], I32, "picked_1")
+        nc.sync.dma_start(out=wc_codes[:], in_=wc_words.rearrange("a p c i -> p a (c i)").bitcast(I32))
+        nc.vector.memset(wc_planes[:], 0)
+        for q in range(QUADS):
+            nc.sync.dma_start(out=wc_planes[32 * q : 32 * q + 2 * QROWS, :], in_=wc_scales.bitcast(I32)[:, QROWS * q : QROWS * (q + 1), :])
+        piece_a(0, 0)
+        for a in range(2):
+            round_wa(1, a, 0, True)
+            round_wa(1, a, 1, False)
+        quantize_wa(1, 0)
+        quantize_wa(1, 1)
+        piece_b(0, 1)
+        piece_a(0, 1)
+        for cols in chunks:
+            group_h(0, 0, cols, True)
+        quantize_h(0, 0, whole)
+        piece_a(1, 0)
+        piece_b(1, 1)
+        for cols in chunks:
+            group_h(0, 1, cols, True)
+        quantize_h(0, 1, whole)
+        group_h(1, 0, chunks[0], False)
+        group_h(1, 0, chunks[1], True)
+        banks = [matmul_a(1, 1, t) for t in range(PACK)]
+        quantize_h(1, 0, whole)
+        logits(0, whole, False)
+        for cols in chunks:
+            for t in range(PACK):
+                maxout(1, 1, t, banks[t], cols)
+            group_h(1, 1, cols, cols is chunks[0])
+            quantize_h(1, 1, cols)
+            logits(1, cols, cols is chunks[-1])

@@ -39,71 +39,72 @@ def tile_list_stroke_maxout_logits_kernel(tc, tab, offs, wa, ba, wb_words, wb_sc
         offsets = lists.tile([P, S // 16], U16, name="offsets")
         tab_scales = held("tab_scales", [P, T // 4], I32)
         tab_words = held("tab_words", [P, T], I32)
-        wb_scales_raw = held("wb_scales_raw", [P, H // 4], I32)
-        wb_raw = [held("wb_raw_%d" % g, [P, 2, PASS // 2], I32) for g in range(2)]
-        wb_planes = held("wb_planes", [P, 2, H // 4], I32)
+        wb_scales_raw = held("wb_scales_raw", [P, 2, H // 4], I32)
+        wb_raw = held("wb_raw", [P, 2, H // 2], I32)
         ba_sb = held("ba_sb", [P, 2, PACK], F32)
         bb_sb = held("bb_sb", [P, 2, PACK], F32)
         bc_sb = held("bc_sb", [P, 2], F32)
-        v_planes = [held("v_planes_%d" % u, [P, 2, HALF // 4], I32) for u in range(2)]
-        wa_raw = {}
+        v_planes = held("v_planes", [P, 2, S // 4], I32)
+        wc_codes = held("wc_codes", [P, 2, N], I32)
+        wc_planes = held("wc_planes", [P, N // 4], I32)
+        pairs = [(i, j) for i in range(2) for j in range(2)]
+        wa_raw = {key: held("wa_raw_%d_%d" % key, [P, PACK, PASS], F32) for key in pairs}
 
-        def load_wa(g, a, tag, pieces=1):
-            wa_raw[g, a] = held("wa_raw_%d_%d" % (g, a), [P, PACK, PASS], F32, tag)
+        def load_wa(g, a, cols):
             rows = wa[PASS * a : PASS * (a + 1), PASS * g : PASS * (g + 1)].rearrange("(p j) c -> p j c", j=PACK)
-            for i in range(pieces):
-                cols = slice(i * PASS // pieces, (i + 1) * PASS // pieces)
-                nc.sync.dma_start(out=wa_raw[g, a][:, :, cols], in_=rows[:, :, cols])
+            nc.sync.dma_start(out=wa_raw[g, a][:, :, cols], in_=rows[:, :, cols])
 
-        def spread_planes(queue, planes, rows):
-            for q in range(QUADS):
-                queue.dma_start(out=planes[32 * q : 32 * q + QROWS, :, :], in_=rows[2 * QROWS * q : 2 * QROWS * (q + 1), :].bitcast(I32))
+        whole = slice(0, HALF)
+        halves = [slice(0, HALF // 2), slice(HALF // 2, HALF)]
 
         nc.sync.dma_start(offsets[:], offs)
         nc.sync.dma_start(out=tab_scales[:ROWS, :], in_=tab[0, 512 * T :].rearrange("(a q t) -> q a t", a=2, q=16).bitcast(I32))
-        nc.sync.dma_start(out=wb_scales_raw[:ROWS, :], in_=wb_scales.bitcast(I32).rearrange("a q c -> q a c"))
-        nc.sync.dma_start(out=tab_words[:], in_=tab[0, : 512 * T].rearrange("(p b) -> p b", p=P).bitcast(I32))
-        for g in range(2):
-            cols = slice(g * PASS // 2, (g + 1) * PASS // 2)
-            nc.sync.dma_start(out=wb_raw[g][:], in_=wb_words.bitcast(I32)[:, :, cols].rearrange("a p c -> p a c"))
-
-        for rows in (wb_scales_raw, tab_scales):
-            nc.vector.memset(rows[ROWS : 2 * ROWS, :], 0)
-            nc.vector.memset(rows[2 * ROWS :, :], 0)
-        nc.vector.memset(wb_planes[:], 0)
-        for u in range(2):
-            nc.vector.memset(v_planes[u][:], 0)
         nc.gpsimd.dma_start(out=bb_sb[:], in_=bb.rearrange("(g p t) -> p g t", g=2, t=PACK))
         nc.gpsimd.dma_start(out=ba_sb[:], in_=ba.rearrange("(g p t) -> p g t", g=2, t=PACK))
         with nc.allow_non_contiguous_dma(reason="one bias value for each partition"):
             nc.gpsimd.dma_start(out=bc_sb[:], in_=bc.rearrange("(c p) -> p c", p=P))
 
-        wb_scale_rows = held("wb_scale_rows", [P, H], U8)
-        nc.vector.tensor_copy(
-            out=wb_scale_rows[:].rearrange("p (g t m) -> p g t m", g=2, t=PACK),
-            in_=wb_scales_raw[:].bitcast(U8).rearrange("p (g m t) -> p g t m", g=2, t=PACK),
-        )
-        spread_planes(nc.sync, wb_planes, wb_scale_rows)
-        load_wa(0, 0, "wb_scales_raw", pieces=2)
+        nc.vector.memset(wb_scales_raw[:], 0)
+        nc.vector.memset(tab_scales[ROWS : 2 * ROWS, :], 0)
+        nc.vector.memset(tab_scales[2 * ROWS :, :], 0)
+        early = held("early", [P, 2], F32)
+        nc.vector.memset(early[:, :1], 0.0)
+        nc.scalar.activation(out=early[:, 1:], in_=early[:, :1], func=IDENTITY)
+        nc.vector.memset(v_planes[:], 0)
+        nc.vector.memset(wc_planes[:], 0)
+
+        for q in range(QUADS):
+            rows = wb_scales.bitcast(I32)[:, QROWS * q : QROWS * (q + 1), :]
+            nc.sync.dma_start(out=wb_scales_raw[32 * q : 32 * q + QROWS, :, :], in_=rows.rearrange("a r c -> r a c"))
+        nc.sync.dma_start(out=tab_words[:], in_=tab[0, : 512 * T].rearrange("(p b) -> p b", p=P).bitcast(I32))
+        nc.sync.dma_start(out=wb_raw[:], in_=wb_words.bitcast(I32).rearrange("a p c -> p a c"))
+        load_wa(0, 0, halves[0])
+
+        picked_scales = held("picked_scales", [P, S], U8)
+        nc.vector.tensor_copy(out=picked_scales[:], in_=tab_scales[:].bitcast(U8).indirect(offsets[:]))
+        for q in range(QUADS):
+            rows = picked_scales[2 * QROWS * q : 2 * QROWS * (q + 1), :]
+            nc.sync.dma_start(out=v_planes[32 * q : 32 * q + QROWS, :, :], in_=rows.bitcast(I32))
+
+        load_wa(0, 0, halves[1])
+        for g, a in pairs[1:]:
+            load_wa(g, a, whole)
+        nc.sync.dma_start(out=wc_codes[:], in_=wc_words.rearrange("a p c i -> p a (c i)").bitcast(I32))
+        for q in range(QUADS):
+            nc.sync.dma_start(out=wc_planes[32 * q : 32 * q + 2 * QROWS, :], in_=wc_scales.bitcast(I32)[:, QROWS * q : QROWS * (q + 1), :])
 
         v_codes = {}
 
-        def gather_scales(u):
-            picked = held("picked_scales_%d" % u, [P, HALF], U8)
-            cols = offsets[:, u * (HALF // 16) : (u + 1) * (HALF // 16)]
-            nc.vector.tensor_copy(out=picked[:], in_=tab_scales[:].bitcast(U8).indirect(cols))
-            spread_planes(nc.scalar, v_planes[u], picked)
-
         def gather_words(u):
-            picked = held("picked_%d" % u, [P, HALF], U32)
+            picked = held("picked_%d" % u, [P, HALF], U32, "picked")
             cols = offsets[:, u * (HALF // 16) : (u + 1) * (HALF // 16)]
             nc.vector.tensor_copy(out=picked[:], in_=tab_words[:].bitcast(U32).indirect(cols))
             parted = held("v_codes_%d" % u, [P, 2, 2 * HALF], U8)
             nc.vector.tensor_copy(out=parted[:].bitcast(U16), in_=picked[:].bitcast(U16).rearrange("p (j a) -> p a j", a=2))
             v_codes[u] = parted
 
-        def v_operand(u, a):
-            return v_codes[u][:, a, :].bitcast(FP4X4), v_planes[u][:, a, :].bitcast(U8)
+        def v_operand(u, a, cols):
+            return v_codes[u][:, a, 2 * cols.start : 2 * cols.stop].bitcast(FP4X4), v_planes[:].bitcast(U8)[:, a, HALF * u + cols.start : HALF * u + cols.stop]
 
         wb_codes = {}
 
@@ -111,10 +112,18 @@ def tile_list_stroke_maxout_logits_kernel(tc, tab, offs, wa, ba, wb_words, wb_sc
             wb_codes[g] = held("wb_codes_%d" % g, [P, 2, 2 * PASS], U8)
             nc.vector.tensor_copy(
                 out=wb_codes[g][:].bitcast(U16).rearrange("p a (t m) -> p a t m", t=PACK),
-                in_=wb_raw[g][:].bitcast(U16).rearrange("p a (m t) -> p a t m", t=PACK),
+                in_=wb_raw[:].bitcast(U16)[:, :, PASS * g : PASS * (g + 1)].rearrange("p a (m t) -> p a t m", t=PACK),
             )
 
-        pairs = [(i, j) for i in range(2) for j in range(2)]
+        wb_planes = {}
+
+        def permute_wb_scales(g, tag):
+            wb_planes[g] = held("wb_planes_%d" % g, [P, 2, PASS], U8, tag)
+            nc.vector.tensor_copy(
+                out=wb_planes[g][:].rearrange("p a (t m) -> p a t m", t=PACK),
+                in_=wb_scales_raw[:].bitcast(U8)[:, :, PASS * g : PASS * (g + 1)].rearrange("p a (m t) -> p a t m", t=PACK),
+            )
+
         wa_bf16 = {key: held("wa_bf16_%d_%d" % key, [P, PACK, P, PACK], BF16) for key in pairs}
         wa_codes = {key: held("wa_codes_%d_%d" % key, [P, PASS], U32) for key in pairs}
         wa_planes = {key: held("wa_planes_%d_%d" % key, [P, PASS], U8) for key in pairs}
@@ -142,11 +151,11 @@ def tile_list_stroke_maxout_logits_kernel(tc, tab, offs, wa, ba, wb_words, wb_sc
             for t in range(PACK):
                 bank = psum.tile([P, HALF], F32, name="scalar_bank", bufs=4)
                 for a in range(2):
-                    codes, plane = v_operand(u, a)
+                    codes, plane = v_operand(u, a, slice(0, HALF))
                     nc.tensor.matmul_mx(
                         out=bank[:],
                         lhsT=wb_codes[g][:, a, 2 * P * t : 2 * P * (t + 1)].bitcast(FP4X4),
-                        lhsT_scale=wb_planes[:].bitcast(U8)[:, a, PASS * g + P * t : PASS * g + P * (t + 1)],
+                        lhsT_scale=wb_planes[g][:, a, P * t : P * (t + 1)],
                         rhs=codes,
                         rhs_scale=plane,
                         start=(a == 0),
@@ -163,7 +172,7 @@ def tile_list_stroke_maxout_logits_kernel(tc, tab, offs, wa, ba, wb_words, wb_sc
         def matmul_a(g, u, t):
             bank = psum.tile([P, HALF], F32, name="a_bank", bufs=4)
             for a in range(2):
-                codes, plane = v_operand(u, a)
+                codes, plane = v_operand(u, a, whole)
                 nc.tensor.matmul_mx(
                     out=bank[:],
                     lhsT=wa_codes[g, a][:, P * t : P * (t + 1)].bitcast(FP8X4),
@@ -225,55 +234,46 @@ def tile_list_stroke_maxout_logits_kernel(tc, tab, offs, wa, ba, wb_words, wb_sc
                     nc.scalar.activation(out=result[:], in_=bank[:, :width], func=IDENTITY, bias=bc_sb[:, c : c + 1])
                 nc.sync.dma_start(out=out[P * c : P * (c + 1), HALF * u + cols.start : HALF * u + cols.stop], in_=result[:])
 
-        whole = slice(0, HALF)
-        chunks = [slice(0, HALF // 2), slice(HALF // 2, HALF)]
-        gather_scales(0)
+        permute_wb_scales(0, "")
         gather_words(0)
         permute_wb(0)
-        load_wa(0, 1, "wb_raw_0")
         permute_wb(1)
         round_wa(0, 0, 0, True)
-        round_wa(0, 0, 1, True)
+        round_wa(0, 0, 1, False)
         piece_b(0, 0)
+        gather_words(1)
+        permute_wb_scales(1, "wb_raw")
         round_wa(0, 1, 0, False)
         round_wa(0, 1, 1, False)
         quantize_wa(0, 0)
-        quantize_wa(0, 1)
         piece_b(1, 0)
-        load_wa(1, 0, "wb_raw_1")
-        gather_scales(1)
-        load_wa(1, 1, "tab_scales")
-        gather_words(1)
-        wc_codes = held("wc_codes", [P, 2, N], I32, "tab_words")
-        wc_planes = held("wc_planes", [P, N // 4], I32, "picked_1")
-        nc.sync.dma_start(out=wc_codes[:], in_=wc_words.rearrange("a p c i -> p a (c i)").bitcast(I32))
-        nc.vector.memset(wc_planes[:], 0)
-        for q in range(QUADS):
-            nc.sync.dma_start(out=wc_planes[32 * q : 32 * q + 2 * QROWS, :], in_=wc_scales.bitcast(I32)[:, QROWS * q : QROWS * (q + 1), :])
+        quantize_wa(0, 1)
+        round_wa(1, 0, 0, True)
+        round_wa(1, 0, 1, False)
         piece_a(0, 0)
-        for a in range(2):
-            round_wa(1, a, 0, True)
-            round_wa(1, a, 1, False)
-        quantize_wa(1, 0)
-        quantize_wa(1, 1)
         piece_b(0, 1)
+        quantize_wa(1, 0)
+        round_wa(1, 1, 0, True)
+        round_wa(1, 1, 1, False)
         piece_a(0, 1)
-        for cols in chunks:
-            group_h(0, 0, cols, True)
-        quantize_h(0, 0, whole)
-        piece_a(1, 0)
+        quantize_wa(1, 1)
         piece_b(1, 1)
-        for cols in chunks:
-            group_h(0, 1, cols, True)
+        piece_a(1, 0)
+        for cols in halves:
+            group_h(0, 0, cols, True)
+        group_h(0, 1, halves[0], False)
+        group_h(0, 1, halves[1], True)
+        quantize_h(0, 0, whole)
         quantize_h(0, 1, whole)
-        group_h(1, 0, chunks[0], False)
-        group_h(1, 0, chunks[1], True)
+        for cols in halves:
+            group_h(1, 0, cols, True)
         banks = [matmul_a(1, 1, t) for t in range(PACK)]
         quantize_h(1, 0, whole)
-        logits(0, whole, False)
-        for cols in chunks:
+        for cols in halves:
             for t in range(PACK):
                 maxout(1, 1, t, banks[t], cols)
-            group_h(1, 1, cols, cols is chunks[0])
+            if cols is halves[0]:
+                logits(0, whole, False)
+            group_h(1, 1, cols, cols is halves[0])
             quantize_h(1, 1, cols)
-            logits(1, cols, cols is chunks[-1])
+            logits(1, cols, cols is halves[1])

@@ -40,7 +40,7 @@ def tile_list_stroke_maxout_logits_kernel(tc, tab, offs, wa, ba, wb_words, wb_sc
         tab_scales = held("tab_scales", [P, T // 4], I32)
         tab_words = held("tab_words", [P, T], I32)
         wb_scales_raw = held("wb_scales_raw", [P, 2, H // 4], I32)
-        wb_raw = held("wb_raw", [P, 2, H // 2], I32)
+        wb_raw = [held("wb_raw_%d" % g, [P, 2, PASS // 2], I32) for g in range(2)]
         ba_sb = held("ba_sb", [P, 2, PACK], F32)
         bb_sb = held("bb_sb", [P, 2, PACK], F32)
         bc_sb = held("bc_sb", [P, 2], F32)
@@ -48,21 +48,22 @@ def tile_list_stroke_maxout_logits_kernel(tc, tab, offs, wa, ba, wb_words, wb_sc
         wc_codes = held("wc_codes", [P, 2, N], I32)
         wc_planes = held("wc_planes", [P, N // 4], I32)
         pairs = [(i, j) for i in range(2) for j in range(2)]
-        wa_raw = {key: held("wa_raw_%d_%d" % key, [P, PACK, PASS], F32) for key in pairs}
+        wa_raw = {(g, a, part): held("wa_raw_%d_%d_%d" % (g, a, part), [P, PACK, PASS // 2], F32) for g, a in pairs for part in range(2)}
 
-        def load_wa(g, a, cols):
-            rows = wa[PASS * a : PASS * (a + 1), PASS * g : PASS * (g + 1)].rearrange("(p j) c -> p j c", j=PACK)
-            nc.sync.dma_start(out=wa_raw[g, a][:, :, cols], in_=rows[:, :, cols])
+        def load_wa(g, a, part):
+            first = PASS * g + part * (PASS // 2)
+            rows = wa[PASS * a : PASS * (a + 1), first : first + PASS // 2].rearrange("(p j) c -> p j c", j=PACK)
+            nc.sync.dma_start(out=wa_raw[g, a, part][:], in_=rows)
+
+        def load_wb(g):
+            words = wb_words.bitcast(I32)[:, :, (PASS // 2) * g : (PASS // 2) * (g + 1)]
+            nc.sync.dma_start(out=wb_raw[g][:], in_=words.rearrange("a p c -> p a c"))
+
+        def load_bias(tile, bias):
+            nc.sync.dma_start(out=tile[:], in_=bias.rearrange("(g p t) -> p g t", g=2, t=PACK))
 
         whole = slice(0, HALF)
         halves = [slice(0, HALF // 2), slice(HALF // 2, HALF)]
-
-        nc.sync.dma_start(offsets[:], offs)
-        nc.sync.dma_start(out=tab_scales[:ROWS, :], in_=tab[0, 512 * T :].rearrange("(a q t) -> q a t", a=2, q=16).bitcast(I32))
-        nc.gpsimd.dma_start(out=bb_sb[:], in_=bb.rearrange("(g p t) -> p g t", g=2, t=PACK))
-        nc.gpsimd.dma_start(out=ba_sb[:], in_=ba.rearrange("(g p t) -> p g t", g=2, t=PACK))
-        with nc.allow_non_contiguous_dma(reason="one bias value for each partition"):
-            nc.gpsimd.dma_start(out=bc_sb[:], in_=bc.rearrange("(c p) -> p c", p=P))
 
         nc.vector.memset(wb_scales_raw[:], 0)
         nc.vector.memset(tab_scales[ROWS : 2 * ROWS, :], 0)
@@ -73,35 +74,40 @@ def tile_list_stroke_maxout_logits_kernel(tc, tab, offs, wa, ba, wb_words, wb_sc
         nc.vector.memset(v_planes[:], 0)
         nc.vector.memset(wc_planes[:], 0)
 
-        for q in range(QUADS):
-            rows = wb_scales.bitcast(I32)[:, QROWS * q : QROWS * (q + 1), :]
-            nc.sync.dma_start(out=wb_scales_raw[32 * q : 32 * q + QROWS, :, :], in_=rows.rearrange("a r c -> r a c"))
-        nc.sync.dma_start(out=tab_words[:], in_=tab[0, : 512 * T].rearrange("(p b) -> p b", p=P).bitcast(I32))
-        nc.sync.dma_start(out=wb_raw[:], in_=wb_words.bitcast(I32).rearrange("a p c -> p a c"))
-        load_wa(0, 0, halves[0])
-
         picked_scales = held("picked_scales", [P, S], U8)
-        nc.vector.tensor_copy(out=picked_scales[:], in_=tab_scales[:].bitcast(U8).indirect(offsets[:]))
-        for q in range(QUADS):
-            rows = picked_scales[2 * QROWS * q : 2 * QROWS * (q + 1), :]
-            nc.sync.dma_start(out=v_planes[32 * q : 32 * q + QROWS, :, :], in_=rows.bitcast(I32))
 
-        load_wa(0, 0, halves[1])
-        for g, a in pairs[1:]:
-            load_wa(g, a, whole)
-        nc.sync.dma_start(out=wc_codes[:], in_=wc_words.rearrange("a p c i -> p a (c i)").bitcast(I32))
-        for q in range(QUADS):
-            nc.sync.dma_start(out=wc_planes[32 * q : 32 * q + 2 * QROWS, :], in_=wc_scales.bitcast(I32)[:, QROWS * q : QROWS * (q + 1), :])
+        def load_head():
+            nc.sync.dma_start(offsets[:], offs)
+            nc.sync.dma_start(out=tab_scales[:ROWS, :], in_=tab[0, 512 * T :].rearrange("(a q t) -> q a t", a=2, q=16).bitcast(I32))
+            load_wb(0)
+            for q in range(QUADS):
+                rows = wb_scales.bitcast(I32)[:, QROWS * q : QROWS * (q + 1), :]
+                nc.sync.dma_start(out=wb_scales_raw[32 * q : 32 * q + QROWS, :, :], in_=rows.rearrange("a r c -> r a c"))
+            nc.sync.dma_start(out=tab_words[:], in_=tab[0, : 512 * T].rearrange("(p b) -> p b", p=P).bitcast(I32))
 
-        v_codes = {}
+        def gather_scales():
+            nc.vector.tensor_copy(out=picked_scales[:], in_=tab_scales[:].bitcast(U8).indirect(offsets[:]))
+            for q in range(QUADS):
+                rows = picked_scales[2 * QROWS * q : 2 * QROWS * (q + 1), :]
+                nc.sync.dma_start(out=v_planes[32 * q : 32 * q + QROWS, :, :], in_=rows.bitcast(I32))
 
-        def gather_words(u):
-            picked = held("picked_%d" % u, [P, HALF], U32, "picked")
-            cols = offsets[:, u * (HALF // 16) : (u + 1) * (HALF // 16)]
-            nc.vector.tensor_copy(out=picked[:], in_=tab_words[:].bitcast(U32).indirect(cols))
-            parted = held("v_codes_%d" % u, [P, 2, 2 * HALF], U8)
-            nc.vector.tensor_copy(out=parted[:].bitcast(U16), in_=picked[:].bitcast(U16).rearrange("p (j a) -> p a j", a=2))
-            v_codes[u] = parted
+        def load_wc():
+            nc.sync.dma_start(out=wc_codes[:], in_=wc_words.rearrange("a p c i -> p a (c i)").bitcast(I32))
+            for q in range(QUADS):
+                nc.sync.dma_start(out=wc_planes[32 * q : 32 * q + 2 * QROWS, :], in_=wc_scales.bitcast(I32)[:, QROWS * q : QROWS * (q + 1), :])
+            with nc.allow_non_contiguous_dma(reason="one bias value for each partition"):
+                nc.sync.dma_start(out=bc_sb[:], in_=bc.rearrange("(c p) -> p c", p=P))
+
+        picked = {}
+        v_codes = [held("v_codes_%d" % u, [P, 2, 2 * HALF], U8) for u in range(2)]
+
+        def gather_words(u, cols, tag):
+            picked[u, cols.start] = held("picked_%d_%d" % (u, cols.start), [P, cols.stop - cols.start], U32, tag)
+            entries = offsets[:, (HALF * u + cols.start) // 16 : (HALF * u + cols.stop) // 16]
+            nc.vector.tensor_copy(out=picked[u, cols.start][:], in_=tab_words[:].bitcast(U32).indirect(entries))
+
+        def part_words(u, cols):
+            nc.vector.tensor_copy(out=v_codes[u][:].bitcast(U16)[:, :, cols], in_=picked[u, cols.start][:].bitcast(U16).rearrange("p (j a) -> p a j", a=2))
 
         def v_operand(u, a, cols):
             return v_codes[u][:, a, 2 * cols.start : 2 * cols.stop].bitcast(FP4X4), v_planes[:].bitcast(U8)[:, a, HALF * u + cols.start : HALF * u + cols.stop]
@@ -112,16 +118,16 @@ def tile_list_stroke_maxout_logits_kernel(tc, tab, offs, wa, ba, wb_words, wb_sc
             wb_codes[g] = held("wb_codes_%d" % g, [P, 2, 2 * PASS], U8)
             nc.vector.tensor_copy(
                 out=wb_codes[g][:].bitcast(U16).rearrange("p a (t m) -> p a t m", t=PACK),
-                in_=wb_raw[:].bitcast(U16)[:, :, PASS * g : PASS * (g + 1)].rearrange("p a (m t) -> p a t m", t=PACK),
+                in_=wb_raw[g][:].bitcast(U16).rearrange("p a (m t) -> p a t m", t=PACK),
             )
 
         wb_planes = {}
 
-        def permute_wb_scales(g, tag):
-            wb_planes[g] = held("wb_planes_%d" % g, [P, 2, PASS], U8, tag)
-            nc.vector.tensor_copy(
-                out=wb_planes[g][:].rearrange("p a (t m) -> p a t m", t=PACK),
-                in_=wb_scales_raw[:].bitcast(U8)[:, :, PASS * g : PASS * (g + 1)].rearrange("p a (m t) -> p a t m", t=PACK),
+        def permute_wb_scales(g, a, tag):
+            wb_planes[g, a] = held("wb_planes_%d_%d" % (g, a), [P, PASS], U8, tag)
+            nc.gpsimd.tensor_copy(
+                out=wb_planes[g, a][:].rearrange("p (t m) -> p t m", t=PACK),
+                in_=wb_scales_raw[:].bitcast(U8)[:, a, PASS * g : PASS * (g + 1)].rearrange("p (m t) -> p t m", t=PACK),
             )
 
         wa_bf16 = {key: held("wa_bf16_%d_%d" % key, [P, PACK, P, PACK], BF16) for key in pairs}
@@ -130,7 +136,7 @@ def tile_list_stroke_maxout_logits_kernel(tc, tab, offs, wa, ba, wb_words, wb_sc
 
         def round_wa(g, a, part, on_scalar):
             m = slice(part * (P // 2), (part + 1) * (P // 2))
-            src = wa_raw[g, a][:].rearrange("p j (m t) -> p m j t", t=PACK)[:, m]
+            src = wa_raw[g, a, part][:].rearrange("p j (m t) -> p m j t", t=PACK)
             dst = wa_bf16[g, a][:].rearrange("p t m j -> p m j t")[:, m]
             if on_scalar:
                 nc.scalar.activation(out=dst, in_=src, func=IDENTITY)
@@ -144,67 +150,62 @@ def tile_list_stroke_maxout_logits_kernel(tc, tab, offs, wa, ba, wb_words, wb_sc
                 in_=wa_bf16[g, a][:].rearrange("p t m j -> p (t m j)"),
             )
 
-        b_sums = {}
+        def new_bank(k):
+            return psum.tile([P, HALF], F32, name="bank_%d" % k)
 
-        def piece_b(g, u):
-            sums = held("b_sums_%d_%d" % (g, u), [P, PACK, HALF], F32)
-            for t in range(PACK):
-                bank = psum.tile([P, HALF], F32, name="scalar_bank", bufs=4)
-                for a in range(2):
-                    codes, plane = v_operand(u, a, slice(0, HALF))
-                    nc.tensor.matmul_mx(
-                        out=bank[:],
-                        lhsT=wb_codes[g][:, a, 2 * P * t : 2 * P * (t + 1)].bitcast(FP4X4),
-                        lhsT_scale=wb_planes[g][:, a, P * t : P * (t + 1)],
-                        rhs=codes,
-                        rhs_scale=plane,
-                        start=(a == 0),
-                        stop=(a == 1),
-                    )
-                nc.scalar.activation(out=sums[:, t, :], in_=bank[:], func=IDENTITY, bias=bb_sb[:, g, t : t + 1])
-            b_sums[g, u] = sums
+        def product(piece, g, u, t, cols, sums, passes=(0, 1)):
+            for a in passes:
+                codes, plane = v_operand(u, a, cols)
+                if piece == "a":
+                    weights = wa_codes[g, a][:, P * t : P * (t + 1)].bitcast(FP8X4)
+                    scale = wa_planes[g, a][:, P * t : P * (t + 1)]
+                else:
+                    weights = wb_codes[g][:, a, 2 * P * t : 2 * P * (t + 1)].bitcast(FP4X4)
+                    scale = wb_planes[g, a][:, P * t : P * (t + 1)]
+                nc.tensor.matmul_mx(out=sums, lhsT=weights, lhsT_scale=scale, rhs=codes, rhs_scale=plane, start=(a == passes[0]), stop=(a == passes[1]))
 
-        h_rows = {(g, u): held("h_rows_%d_%d" % (g, u), [P, PACK, HALF], BF16) for g in range(2) for u in range(2)}
-        h_grouped = {key: held("h_grouped_%d_%d" % key, [P, HALF, PACK], BF16) for key in h_rows}
-        h_codes = {key: held("h_codes_%d_%d" % key, [P, HALF], U32) for key in h_rows}
-        h_planes = {key: held("h_planes_%d_%d" % key, [P, HALF], U8) for key in h_rows}
+        bias_of = {"a": ba_sb, "b": bb_sb}
+        reuse = {(0, 0): "wa_raw_0_0_1", (1, 0): "wa_raw_1_0_1"}
+        first_sums = {key: held("first_sums_%d_%d" % key, [P, PACK, HALF], F32, reuse.get(key, "")) for key in pairs}
+        h_rows = {key: held("h_rows_%d_%d" % key, [P, PACK, HALF], BF16, "wa_raw_1_0_0" if key == (0, 0) else "") for key in pairs}
+        h_grouped = {key: held("h_grouped_%d_%d" % key, [P, HALF, PACK], BF16) for key in pairs}
+        h_codes = {key: held("h_codes_%d_%d" % key, [P, HALF], U32) for key in pairs}
+        h_planes = {key: held("h_planes_%d_%d" % key, [P, HALF], U8) for key in pairs}
 
-        def matmul_a(g, u, t):
-            bank = psum.tile([P, HALF], F32, name="a_bank", bufs=4)
-            for a in range(2):
-                codes, plane = v_operand(u, a, whole)
-                nc.tensor.matmul_mx(
-                    out=bank[:],
-                    lhsT=wa_codes[g, a][:, P * t : P * (t + 1)].bitcast(FP8X4),
-                    lhsT_scale=wa_planes[g, a][:, P * t : P * (t + 1)],
-                    rhs=codes,
-                    rhs_scale=plane,
-                    start=(a == 0),
-                    stop=(a == 1),
-                )
-            return bank
+        def first_piece(piece, g, u, t, k, passes=(0, 1)):
+            bank = new_bank(k)
+            product(piece, g, u, t, whole, bank[:], passes)
+            nc.scalar.activation(out=first_sums[g, u][:, t, :], in_=bank[:], func=IDENTITY, bias=bias_of[piece][:, g, t : t + 1])
 
-        def maxout(g, u, t, bank, cols):
+        def maxout(piece, g, u, t, sums, cols):
             nc.vector.scalar_tensor_tensor(
                 out=h_rows[g, u][:, t, cols],
-                in0=bank[:, cols],
-                scalar=ba_sb[:, g, t : t + 1],
-                in1=b_sums[g, u][:, t, cols],
+                in0=sums,
+                scalar=bias_of[piece][:, g, t : t + 1],
+                in1=first_sums[g, u][:, t, cols],
                 op0=ADD,
                 op1=MAX,
             )
 
-        def piece_a(g, u):
-            for t in range(PACK):
-                maxout(g, u, t, matmul_a(g, u, t), slice(0, HALF))
+        def second_piece(piece, g, u, t, k, passes=(0, 1)):
+            bank = new_bank(k)
+            product(piece, g, u, t, whole, bank[:], passes)
+            maxout(piece, g, u, t, bank[:], whole)
 
-        def group_h(g, u, cols, on_scalar):
+        def second_piece_narrow(piece, g, u, pair, cols, k):
+            bank = new_bank(k)
+            for i in range(2):
+                product(piece, g, u, 2 * pair + i, cols, bank[:, halves[i]])
+            for i in range(2):
+                maxout(piece, g, u, 2 * pair + i, bank[:, halves[i]], cols)
+
+        def group_h(g, u, cols, on_scalar, engine=nc.vector):
             src = h_rows[g, u][:, :, cols].rearrange("p t (c i) -> p c t i", i=4)
             dst = h_grouped[g, u][:, cols, :].rearrange("p (c i) t -> p c t i", i=4)
             if on_scalar:
                 nc.scalar.copy(out=dst, in_=src)
             else:
-                nc.vector.tensor_copy(out=dst, in_=src)
+                engine.tensor_copy(out=dst, in_=src)
 
         def quantize_h(g, u, cols):
             nc.vector.quantize_mx(
@@ -213,10 +214,10 @@ def tile_list_stroke_maxout_logits_kernel(tc, tab, offs, wa, ba, wb_words, wb_sc
                 in_=h_grouped[g, u][:, cols, :].rearrange("p j t -> p (j t)"),
             )
 
-        def logits(u, cols, both_engines):
+        def logits(u, cols, both_engines, k):
             width = cols.stop - cols.start
             for c in range(N // P):
-                bank = psum.tile([P, HALF], F32, name="scalar_bank", bufs=4)
+                bank = new_bank(k + c)
                 for g in range(2):
                     nc.tensor.matmul_mx(
                         out=bank[:, :width],
@@ -234,46 +235,86 @@ def tile_list_stroke_maxout_logits_kernel(tc, tab, offs, wa, ba, wb_words, wb_sc
                     nc.scalar.activation(out=result[:], in_=bank[:, :width], func=IDENTITY, bias=bc_sb[:, c : c + 1])
                 nc.sync.dma_start(out=out[P * c : P * (c + 1), HALF * u + cols.start : HALF * u + cols.stop], in_=result[:])
 
-        permute_wb_scales(0, "")
-        gather_words(0)
+        load_head()
+        load_wa(0, 0, 0)
+        load_wb(1)
+        load_bias(bb_sb, bb)
+        gather_scales()
+        load_wa(0, 0, 1)
+        load_wa(0, 1, 0)
+        load_wa(0, 1, 1)
+        load_bias(ba_sb, ba)
+        load_wa(1, 0, 0)
+        load_wa(1, 0, 1)
+        load_wa(1, 1, 0)
+        load_wa(1, 1, 1)
+        load_wc()
+
+        permute_wb_scales(0, 0, "")
+        permute_wb_scales(0, 1, "")
         permute_wb(0)
-        permute_wb(1)
+        permute_wb_scales(1, 0, "wb_raw_0")
+        gather_words(0, halves[0], "picked")
+        gather_words(0, halves[1], "picked_second")
+        part_words(0, halves[0])
+        part_words(0, halves[1])
         round_wa(0, 0, 0, True)
-        round_wa(0, 0, 1, False)
-        piece_b(0, 0)
-        gather_words(1)
-        permute_wb_scales(1, "wb_raw")
+        round_wa(0, 0, 1, True)
+        permute_wb_scales(1, 1, "picked_second")
+        gather_words(1, whole, "picked")
+        part_words(1, whole)
+        for t in range(PACK):
+            first_piece("b", 0, 0, t, t)
+        quantize_wa(0, 0)
         round_wa(0, 1, 0, False)
         round_wa(0, 1, 1, False)
-        quantize_wa(0, 0)
-        piece_b(1, 0)
+        permute_wb(1)
         quantize_wa(0, 1)
-        round_wa(1, 0, 0, True)
-        round_wa(1, 0, 1, False)
-        piece_a(0, 0)
-        piece_b(0, 1)
+        for t in range(PACK):
+            first_piece("b", 0, 1, t, PACK + t)
+        round_wa(1, 0, 0, False)
+        round_wa(1, 0, 1, True)
+        second_piece("a", 0, 0, 0, 0)
+        second_piece("a", 0, 0, 1, 1)
+        first_piece("b", 1, 0, 0, 2)
         quantize_wa(1, 0)
+        second_piece("a", 0, 0, 2, 3)
         round_wa(1, 1, 0, True)
+        first_piece("b", 1, 0, 1, 4)
+        second_piece("a", 0, 0, 3, 5)
         round_wa(1, 1, 1, False)
-        piece_a(0, 1)
+        first_piece("b", 1, 0, 2, 6)
+        second_piece("a", 0, 1, 0, 7)
+        first_piece("b", 1, 0, 3, 0)
         quantize_wa(1, 1)
-        piece_b(1, 1)
-        piece_a(1, 0)
-        for cols in halves:
-            group_h(0, 0, cols, True)
-        group_h(0, 1, halves[0], False)
-        group_h(0, 1, halves[1], True)
+        group_h(0, 0, halves[0], True)
+        second_piece("a", 0, 1, 1, 1)
+        second_piece("a", 0, 1, 2, 2)
+        group_h(0, 0, halves[1], True)
+        second_piece("a", 0, 1, 3, 3)
+        second_piece("a", 1, 0, 0, 4)
+        first_piece("a", 1, 1, 0, 5)
+        group_h(0, 1, halves[0], True)
         quantize_h(0, 0, whole)
-        quantize_h(0, 1, whole)
-        for cols in halves:
-            group_h(1, 0, cols, True)
-        banks = [matmul_a(1, 1, t) for t in range(PACK)]
+        second_piece("a", 1, 0, 1, 6)
+        first_piece("a", 1, 1, 1, 7)
+        second_piece("a", 1, 0, 2, 0)
+        first_piece("a", 1, 1, 2, 1)
+        second_piece("a", 1, 0, 3, 2)
+        first_piece("a", 1, 1, 3, 3)
+        group_h(1, 0, halves[0], False)
+        group_h(1, 0, halves[1], True)
+        group_h(0, 1, halves[1], True)
+        for pair in range(2):
+            second_piece_narrow("b", 1, 1, pair, halves[0], 4 + pair)
         quantize_h(1, 0, whole)
-        for cols in halves:
-            for t in range(PACK):
-                maxout(1, 1, t, banks[t], cols)
-            if cols is halves[0]:
-                logits(0, whole, False)
-            group_h(1, 1, cols, cols is halves[0])
-            quantize_h(1, 1, cols)
-            logits(1, cols, cols is halves[1])
+        group_h(1, 1, halves[0], True)
+        for pair in range(2):
+            second_piece_narrow("b", 1, 1, pair, halves[1], 6 + pair)
+        logits(0, whole, False, 0)
+        quantize_h(0, 1, whole)
+        group_h(1, 1, halves[1], False)
+        quantize_h(1, 1, halves[0])
+        logits(1, halves[0], False, 2)
+        quantize_h(1, 1, halves[1])
+        logits(1, halves[1], True, 4)

@@ -254,6 +254,17 @@ def tile_list_stroke_maxout_logits_kernel(tc, tab, offs, wa, ba, wb_words, wb_sc
         permute_wb_scales(0, 1, "")
         permute_wb(0)
         permute_wb_scales(1, 0, "wb_raw_0")
+        warm = new_bank(7)
+        for i in range(4):
+            nc.tensor.matmul_mx(
+                out=warm[:],
+                lhsT=wb_codes[0][:, 0, : 2 * P].bitcast(FP4X4),
+                lhsT_scale=wb_planes[0, 0][:, :P],
+                rhs=wb_codes[0][:, 0, :].bitcast(FP4X4),
+                rhs_scale=wb_planes[0, 0][:],
+                start=True,
+                stop=True,
+            )
         gather_words(0, halves[0], "picked")
         gather_words(0, halves[1], "picked_second")
         part_words(0, halves[0])

@@ -16,6 +16,7 @@ FP4X4 = mybir.dt.float4_e2m1fn_x4
 IDENTITY = mybir.ActivationFunctionType.Identity
 ADD = mybir.AluOpType.add
 MAX = mybir.AluOpType.max
+MULT = mybir.AluOpType.mult
 
 P = 128
 PACK = 4
@@ -23,7 +24,12 @@ PASS = P * PACK
 QUADS = 4
 QROWS = 4
 HALF = 512
+TABLE_WORD_BYTES = 4 * P * T
 ROWS = 32
+LIST_ROWS = 16
+BANKS = 8
+RUN = 4
+WARM_UP = 4
 
 
 def tile_list_stroke_maxout_logits_kernel(tc, tab, offs, wa, ba, wb_words, wb_scales, bb, wc_words, wc_scales, bc, out):
@@ -36,7 +42,7 @@ def tile_list_stroke_maxout_logits_kernel(tc, tab, offs, wa, ba, wb_words, wb_sc
         def held(name, shape, dtype, tag=""):
             return keep.tile(shape, dtype, name=name, tag=tag or name, align_bytes=64)
 
-        offsets = lists.tile([P, S // 16], U16, name="offsets")
+        offsets = lists.tile([P, S // LIST_ROWS], U16, name="offsets")
         tab_scales = held("tab_scales", [P, T // 4], I32)
         tab_words = held("tab_words", [P, T], I32)
         wb_scales_raw = held("wb_scales_raw", [P, 2, H // 4], I32)
@@ -78,12 +84,12 @@ def tile_list_stroke_maxout_logits_kernel(tc, tab, offs, wa, ba, wb_words, wb_sc
 
         def load_head():
             nc.sync.dma_start(offsets[:], offs)
-            nc.sync.dma_start(out=tab_scales[:ROWS, :], in_=tab[0, 512 * T :].rearrange("(a q t) -> q a t", a=2, q=16).bitcast(I32))
+            nc.sync.dma_start(out=tab_scales[:ROWS, :], in_=tab[0, TABLE_WORD_BYTES:].rearrange("(a n c) -> n a c", a=2, n=ROWS // 2).bitcast(I32))
             load_wb(0)
             for q in range(QUADS):
                 rows = wb_scales.bitcast(I32)[:, QROWS * q : QROWS * (q + 1), :]
-                nc.sync.dma_start(out=wb_scales_raw[32 * q : 32 * q + QROWS, :, :], in_=rows.rearrange("a r c -> r a c"))
-            nc.sync.dma_start(out=tab_words[:], in_=tab[0, : 512 * T].rearrange("(p b) -> p b", p=P).bitcast(I32))
+                nc.sync.dma_start(out=wb_scales_raw[32 * q : 32 * q + QROWS, :, :], in_=rows.rearrange("a w c -> w a c"))
+            nc.sync.dma_start(out=tab_words[:], in_=tab[0, :TABLE_WORD_BYTES].rearrange("(p b) -> p b", p=P).bitcast(I32))
 
         def gather_scales():
             nc.vector.tensor_copy(out=picked_scales[:], in_=tab_scales[:].bitcast(U8).indirect(offsets[:]))
@@ -103,7 +109,7 @@ def tile_list_stroke_maxout_logits_kernel(tc, tab, offs, wa, ba, wb_words, wb_sc
 
         def gather_words(u, cols, tag):
             picked[u, cols.start] = held("picked_%d_%d" % (u, cols.start), [P, cols.stop - cols.start], U32, tag)
-            entries = offsets[:, (HALF * u + cols.start) // 16 : (HALF * u + cols.stop) // 16]
+            entries = offsets[:, (HALF * u + cols.start) // LIST_ROWS : (HALF * u + cols.stop) // LIST_ROWS]
             nc.vector.tensor_copy(out=picked[u, cols.start][:], in_=tab_words[:].bitcast(U32).indirect(entries))
 
         def part_words(u, cols):
@@ -114,7 +120,7 @@ def tile_list_stroke_maxout_logits_kernel(tc, tab, offs, wa, ba, wb_words, wb_sc
 
         wb_codes = {}
 
-        def permute_wb(g):
+        def reorder_wb(g):
             wb_codes[g] = held("wb_codes_%d" % g, [P, 2, 2 * PASS], U8)
             nc.vector.tensor_copy(
                 out=wb_codes[g][:].bitcast(U16).rearrange("p a (t m) -> p a t m", t=PACK),
@@ -123,9 +129,9 @@ def tile_list_stroke_maxout_logits_kernel(tc, tab, offs, wa, ba, wb_words, wb_sc
 
         wb_planes = {}
 
-        def permute_wb_scales(g, a, tag):
+        def reorder_wb_scales(g, a, engine, tag=""):
             wb_planes[g, a] = held("wb_planes_%d_%d" % (g, a), [P, PASS], U8, tag)
-            nc.gpsimd.tensor_copy(
+            engine.tensor_copy(
                 out=wb_planes[g, a][:].rearrange("p (t m) -> p t m", t=PACK),
                 in_=wb_scales_raw[:].bitcast(U8)[:, a, PASS * g : PASS * (g + 1)].rearrange("p (m t) -> p t m", t=PACK),
             )
@@ -150,8 +156,8 @@ def tile_list_stroke_maxout_logits_kernel(tc, tab, offs, wa, ba, wb_words, wb_sc
                 in_=wa_bf16[g, a][:].rearrange("p t m j -> p (t m j)"),
             )
 
-        def new_bank(k):
-            return psum.tile([P, HALF], F32, name="bank_%d" % k)
+        def new_bank(number):
+            return psum.tile([P, HALF], F32, name="bank_%d" % (number % BANKS))
 
         def product(piece, g, u, t, cols, sums, passes=(0, 1)):
             for a in passes:
@@ -165,15 +171,15 @@ def tile_list_stroke_maxout_logits_kernel(tc, tab, offs, wa, ba, wb_words, wb_sc
                 nc.tensor.matmul_mx(out=sums, lhsT=weights, lhsT_scale=scale, rhs=codes, rhs_scale=plane, start=(a == passes[0]), stop=(a == passes[1]))
 
         bias_of = {"a": ba_sb, "b": bb_sb}
-        reuse = {(0, 0): "wa_raw_0_0_1", (1, 0): "wa_raw_1_0_1"}
-        first_sums = {key: held("first_sums_%d_%d" % key, [P, PACK, HALF], F32, reuse.get(key, "")) for key in pairs}
+        sums_buffer = {(0, 0): "wa_raw_0_0_1", (1, 0): "wa_raw_1_0_1"}
+        first_sums = {key: held("first_sums_%d_%d" % key, [P, PACK, HALF], F32, sums_buffer.get(key, "")) for key in pairs}
         h_rows = {key: held("h_rows_%d_%d" % key, [P, PACK, HALF], BF16, "wa_raw_1_0_0" if key == (0, 0) else "") for key in pairs}
         h_grouped = {key: held("h_grouped_%d_%d" % key, [P, HALF, PACK], BF16) for key in pairs}
-        h_codes = {key: held("h_codes_%d_%d" % key, [P, HALF], U32) for key in pairs}
+        h_codes = {key: held("h_codes_%d_%d" % key, [P, HALF], U32, sums_buffer[1, 0] if key == (0, 0) else "") for key in pairs}
         h_planes = {key: held("h_planes_%d_%d" % key, [P, HALF], U8) for key in pairs}
 
-        def first_piece(piece, g, u, t, k, passes=(0, 1)):
-            bank = new_bank(k)
+        def first_piece(piece, g, u, t, bank_number, passes=(0, 1)):
+            bank = new_bank(bank_number)
             product(piece, g, u, t, whole, bank[:], passes)
             nc.scalar.activation(out=first_sums[g, u][:, t, :], in_=bank[:], func=IDENTITY, bias=bias_of[piece][:, g, t : t + 1])
 
@@ -187,25 +193,30 @@ def tile_list_stroke_maxout_logits_kernel(tc, tab, offs, wa, ba, wb_words, wb_sc
                 op1=MAX,
             )
 
-        def second_piece(piece, g, u, t, k, passes=(0, 1)):
-            bank = new_bank(k)
-            product(piece, g, u, t, whole, bank[:], passes)
+        def second_piece(piece, g, u, t, bank_number):
+            bank = new_bank(bank_number)
+            product(piece, g, u, t, whole, bank[:])
             maxout(piece, g, u, t, bank[:], whole)
 
-        def second_piece_narrow(piece, g, u, pair, cols, k):
-            bank = new_bank(k)
+        def second_piece_narrow(piece, g, u, pair, cols, bank_number):
+            bank = new_bank(bank_number)
             for i in range(2):
                 product(piece, g, u, 2 * pair + i, cols, bank[:, halves[i]])
             for i in range(2):
                 maxout(piece, g, u, 2 * pair + i, bank[:, halves[i]], cols)
 
-        def group_h(g, u, cols, on_scalar, engine=nc.vector):
-            src = h_rows[g, u][:, :, cols].rearrange("p t (c i) -> p c t i", i=4)
-            dst = h_grouped[g, u][:, cols, :].rearrange("p (c i) t -> p c t i", i=4)
+        def group_h(g, u, cols, on_scalar):
+            src = h_rows[g, u][:, :, cols].rearrange("p t (c i) -> p c t i", i=RUN)
+            dst = h_grouped[g, u][:, cols, :].rearrange("p (c i) t -> p c t i", i=RUN)
             if on_scalar:
                 nc.scalar.copy(out=dst, in_=src)
             else:
-                engine.tensor_copy(out=dst, in_=src)
+                nc.vector.tensor_copy(out=dst, in_=src)
+
+        def group_h_on_gpsimd(g, u, cols):
+            nc.gpsimd.tensor_scalar(
+                out=h_grouped[g, u][:, cols, :], in0=h_rows[g, u][:, :, cols].rearrange("p t c -> p c t"), scalar1=1.0, scalar2=0.0, op0=MULT, op1=ADD
+            )
 
         def quantize_h(g, u, cols):
             nc.vector.quantize_mx(
@@ -214,10 +225,10 @@ def tile_list_stroke_maxout_logits_kernel(tc, tab, offs, wa, ba, wb_words, wb_sc
                 in_=h_grouped[g, u][:, cols, :].rearrange("p j t -> p (j t)"),
             )
 
-        def logits(u, cols, both_engines, k):
+        def logits(u, cols, both_engines, bank_number):
             width = cols.stop - cols.start
             for c in range(N // P):
-                bank = new_bank(k + c)
+                bank = new_bank(bank_number + c)
                 for g in range(2):
                     nc.tensor.matmul_mx(
                         out=bank[:, :width],
@@ -241,21 +252,18 @@ def tile_list_stroke_maxout_logits_kernel(tc, tab, offs, wa, ba, wb_words, wb_sc
         load_bias(bb_sb, bb)
         gather_scales()
         load_wa(0, 0, 1)
-        load_wa(0, 1, 0)
-        load_wa(0, 1, 1)
-        load_bias(ba_sb, ba)
-        load_wa(1, 0, 0)
-        load_wa(1, 0, 1)
-        load_wa(1, 1, 0)
-        load_wa(1, 1, 1)
+        for g, a in pairs[1:]:
+            for part in range(2):
+                load_wa(g, a, part)
+            if g == 0:
+                load_bias(ba_sb, ba)
         load_wc()
 
-        permute_wb_scales(0, 0, "")
-        permute_wb_scales(0, 1, "")
-        permute_wb(0)
-        permute_wb_scales(1, 0, "wb_raw_0")
-        warm = new_bank(7)
-        for i in range(4):
+        reorder_wb(0)
+        reorder_wb_scales(0, 0, nc.vector)
+        reorder_wb_scales(0, 1, nc.gpsimd, "wb_raw_0")
+        warm = new_bank(BANKS - 1)
+        for i in range(WARM_UP):
             nc.tensor.matmul_mx(
                 out=warm[:],
                 lhsT=wb_codes[0][:, 0, : 2 * P].bitcast(FP4X4),
@@ -267,65 +275,66 @@ def tile_list_stroke_maxout_logits_kernel(tc, tab, offs, wa, ba, wb_words, wb_sc
             )
         gather_words(0, halves[0], "picked")
         gather_words(0, halves[1], "picked_second")
-        part_words(0, halves[0])
-        part_words(0, halves[1])
-        round_wa(0, 0, 0, True)
-        round_wa(0, 0, 1, True)
-        permute_wb_scales(1, 1, "picked_second")
+        for cols in halves:
+            part_words(0, cols)
+        for part in range(2):
+            round_wa(0, 0, part, on_scalar=True)
+        reorder_wb_scales(1, 0, nc.gpsimd, "picked_second")
         gather_words(1, whole, "picked")
         part_words(1, whole)
+
         for t in range(PACK):
             first_piece("b", 0, 0, t, t)
         quantize_wa(0, 0)
-        round_wa(0, 1, 0, False)
-        round_wa(0, 1, 1, False)
-        permute_wb(1)
+        for part in range(2):
+            round_wa(0, 1, part, on_scalar=False)
+        reorder_wb(1)
+        reorder_wb_scales(1, 1, nc.vector, "picked")
         quantize_wa(0, 1)
         for t in range(PACK):
             first_piece("b", 0, 1, t, PACK + t)
-        round_wa(1, 0, 0, False)
-        round_wa(1, 0, 1, True)
-        second_piece("a", 0, 0, 0, 0)
-        second_piece("a", 0, 0, 1, 1)
-        first_piece("b", 1, 0, 0, 2)
-        quantize_wa(1, 0)
-        second_piece("a", 0, 0, 2, 3)
-        round_wa(1, 1, 0, True)
-        first_piece("b", 1, 0, 1, 4)
-        second_piece("a", 0, 0, 3, 5)
-        round_wa(1, 1, 1, False)
-        first_piece("b", 1, 0, 2, 6)
-        second_piece("a", 0, 1, 0, 7)
-        first_piece("b", 1, 0, 3, 0)
-        quantize_wa(1, 1)
-        group_h(0, 0, halves[0], True)
-        second_piece("a", 0, 1, 1, 1)
-        second_piece("a", 0, 1, 2, 2)
-        group_h(0, 0, halves[1], True)
-        second_piece("a", 0, 1, 3, 3)
-        second_piece("a", 1, 0, 0, 4)
-        first_piece("a", 1, 1, 0, 5)
-        group_h(0, 1, halves[0], True)
+        round_wa(1, 0, 0, on_scalar=False)
+        round_wa(1, 0, 1, on_scalar=True)
+
+        prepare = [
+            lambda: quantize_wa(1, 0),
+            lambda: round_wa(1, 1, 0, on_scalar=True),
+            lambda: round_wa(1, 1, 1, on_scalar=False),
+            lambda: quantize_wa(1, 1),
+        ]
+        bank_number = 0
+        for step in range(2 * PACK):
+            second_piece("a", 0, step // PACK, step % PACK, bank_number)
+            bank_number += 1
+            if 1 <= step <= PACK:
+                prepare[step - 1]()
+                first_piece("b", 1, 0, step - 1, bank_number)
+                bank_number += 1
+        for cols in halves:
+            group_h(0, 0, cols, on_scalar=True)
+        group_h(0, 1, halves[0], on_scalar=True)
+        group_h_on_gpsimd(0, 1, halves[1])
+
+        for t in range(PACK):
+            second_piece("a", 1, 0, t, bank_number + 2 * t)
+            if t == 1:
+                first_piece("a", 1, 1, 0, bank_number + 1, (1, 0))
+        for t in range(1, PACK):
+            first_piece("a", 1, 1, t, bank_number + 2 * t + 1, (1, 0))
         quantize_h(0, 0, whole)
-        second_piece("a", 1, 0, 1, 6)
-        first_piece("a", 1, 1, 1, 7)
-        second_piece("a", 1, 0, 2, 0)
-        first_piece("a", 1, 1, 2, 1)
-        second_piece("a", 1, 0, 3, 2)
-        first_piece("a", 1, 1, 3, 3)
-        group_h(1, 0, halves[0], False)
-        group_h(1, 0, halves[1], True)
-        group_h(0, 1, halves[1], True)
+        group_h(1, 0, halves[0], on_scalar=False)
+        group_h(1, 0, halves[1], on_scalar=True)
+
         for pair in range(2):
-            second_piece_narrow("b", 1, 1, pair, halves[0], 4 + pair)
+            second_piece_narrow("b", 1, 1, pair, halves[0], PACK + pair)
         quantize_h(1, 0, whole)
-        group_h(1, 1, halves[0], True)
+        group_h(1, 1, halves[0], on_scalar=True)
         for pair in range(2):
-            second_piece_narrow("b", 1, 1, pair, halves[1], 6 + pair)
+            second_piece_narrow("b", 1, 1, pair, halves[1], PACK + 2 + pair)
         logits(0, whole, False, 0)
         quantize_h(0, 1, whole)
-        group_h(1, 1, halves[1], False)
+        group_h(1, 1, halves[1], on_scalar=False)
         quantize_h(1, 1, halves[0])
         logits(1, halves[0], False, 2)
         quantize_h(1, 1, halves[1])
-        logits(1, halves[1], True, 4)
+        logits(1, halves[1], True, PACK)

@@ -40,7 +40,7 @@ def tile_list_stroke_maxout_logits_kernel(tc, tab, offs, wa, ba, wb_words, wb_sc
         psum = ctx.enter_context(tc.psum_pool(name="psum", bufs=1))
 
         def held(name, shape, dtype, tag=""):
-            return keep.tile(shape, dtype, name=name, tag=tag or name, align_bytes=64)
+            return keep.tile(shape, dtype, name=name, tag=tag or name, align_bytes=256)
 
         offsets = lists.tile([P, S // LIST_ROWS], U16, name="offsets")
         tab_scales = held("tab_scales", [P, T // 4], I32)

@@ -66,7 +66,7 @@ def tile_list_stroke_maxout_logits_kernel(tc, tab, offs, wa, ba, wb_words, wb_sc
             nc.sync.dma_start(out=wb_raw[g][:], in_=words.rearrange("a p c -> p a c"))
 
         def load_bias(tile, bias):
-            nc.sync.dma_start(out=tile[:], in_=bias.rearrange("(g p t) -> p g t", g=2, t=PACK))
+            nc.gpsimd.dma_start(out=tile[:], in_=bias.rearrange("(g p t) -> p g t", g=2, t=PACK))
 
         whole = slice(0, HALF)
         halves = [slice(0, HALF // 2), slice(HALF // 2, HALF)]
@@ -246,17 +246,17 @@ def tile_list_stroke_maxout_logits_kernel(tc, tab, offs, wa, ba, wb_words, wb_sc
                     nc.scalar.activation(out=result[:], in_=bank[:, :width], func=IDENTITY, bias=bc_sb[:, c : c + 1])
                 nc.sync.dma_start(out=out[P * c : P * (c + 1), HALF * u + cols.start : HALF * u + cols.stop], in_=result[:])
 
+        load_bias(bb_sb, bb)
+        load_bias(ba_sb, ba)
         load_head()
         load_wa(0, 0, 0)
-        load_wb(1)
-        load_bias(bb_sb, bb)
         gather_scales()
         load_wa(0, 0, 1)
         for g, a in pairs[1:]:
             for part in range(2):
                 load_wa(g, a, part)
             if g == 0:
-                load_bias(ba_sb, ba)
+                load_wb(1)
         load_wc()
 
         reorder_wb(0)

@@ -29,7 +29,7 @@ ROWS = 32
 LIST_ROWS = 16
 BANKS = 8
 RUN = 4
-WARM_UP = 4
+WARM_UP = 6
 
 
 def tile_list_stroke_maxout_logits_kernel(tc, tab, offs, wa, ba, wb_words, wb_scales, bb, wc_words, wc_scales, bc, out):
@@ -105,7 +105,7 @@ def tile_list_stroke_maxout_logits_kernel(tc, tab, offs, wa, ba, wb_words, wb_sc
                 nc.sync.dma_start(out=bc_sb[:], in_=bc.rearrange("(c p) -> p c", p=P))
 
         picked = {}
-        v_codes = [held("v_codes_%d" % u, [P, 2, 2 * HALF], U8) for u in range(2)]
+        v_codes = [held("v_codes_%d" % u, [P, 2, HALF], U16) for u in range(2)]
 
         def gather_words(u, cols, tag):
             picked[u, cols.start] = held("picked_%d_%d" % (u, cols.start), [P, cols.stop - cols.start], U32, tag)
@@ -113,10 +113,10 @@ def tile_list_stroke_maxout_logits_kernel(tc, tab, offs, wa, ba, wb_words, wb_sc
             nc.vector.tensor_copy(out=picked[u, cols.start][:], in_=tab_words[:].bitcast(U32).indirect(entries))
 
         def part_words(u, cols):
-            nc.vector.tensor_copy(out=v_codes[u][:].bitcast(U16)[:, :, cols], in_=picked[u, cols.start][:].bitcast(U16).rearrange("p (j a) -> p a j", a=2))
+            nc.vector.tensor_copy(out=v_codes[u][:, :, cols], in_=picked[u, cols.start][:].bitcast(U16).rearrange("p (j a) -> p a j", a=2))
 
         def v_operand(u, a, cols):
-            return v_codes[u][:, a, 2 * cols.start : 2 * cols.stop].bitcast(FP4X4), v_planes[:].bitcast(U8)[:, a, HALF * u + cols.start : HALF * u + cols.stop]
+            return v_codes[u][:, a, cols].bitcast(FP4X4), v_planes[:].bitcast(U8)[:, a, HALF * u + cols.start : HALF * u + cols.stop]
 
         wb_codes = {}
 
@@ -174,14 +174,17 @@ def tile_list_stroke_maxout_logits_kernel(tc, tab, offs, wa, ba, wb_words, wb_sc
         sums_buffer = {(0, 0): "wa_raw_0_0_1", (1, 0): "wa_raw_1_0_1"}
         first_sums = {key: held("first_sums_%d_%d" % key, [P, PACK, HALF], F32, sums_buffer.get(key, "")) for key in pairs}
         h_rows = {key: held("h_rows_%d_%d" % key, [P, PACK, HALF], BF16, "wa_raw_1_0_0" if key == (0, 0) else "") for key in pairs}
-        h_grouped = {key: held("h_grouped_%d_%d" % key, [P, HALF, PACK], BF16) for key in pairs}
+        h_grouped = {key: held("h_grouped_%d_%d" % key, [P, HALF, PACK], BF16, "h_grouped_0_0" if key == (1, 0) else "") for key in pairs}
         h_codes = {key: held("h_codes_%d_%d" % key, [P, HALF], U32, sums_buffer[1, 0] if key == (0, 0) else "") for key in pairs}
         h_planes = {key: held("h_planes_%d_%d" % key, [P, HALF], U8) for key in pairs}
+
+        def take_out(piece, g, u, t, bank):
+            nc.scalar.activation(out=first_sums[g, u][:, t, :], in_=bank[:], func=IDENTITY, bias=bias_of[piece][:, g, t : t + 1])
 
         def first_piece(piece, g, u, t, bank_number, passes=(0, 1)):
             bank = new_bank(bank_number)
             product(piece, g, u, t, whole, bank[:], passes)
-            nc.scalar.activation(out=first_sums[g, u][:, t, :], in_=bank[:], func=IDENTITY, bias=bias_of[piece][:, g, t : t + 1])
+            take_out(piece, g, u, t, bank)
 
         def maxout(piece, g, u, t, sums, cols):
             nc.vector.scalar_tensor_tensor(
@@ -259,24 +262,27 @@ def tile_list_stroke_maxout_logits_kernel(tc, tab, offs, wa, ba, wb_words, wb_sc
                 load_wb(1)
         load_wc()
 
-        reorder_wb(0)
-        reorder_wb_scales(0, 0, nc.vector)
-        reorder_wb_scales(0, 1, nc.gpsimd, "wb_raw_0")
         warm = new_bank(BANKS - 1)
         for i in range(WARM_UP):
             nc.tensor.matmul_mx(
                 out=warm[:],
-                lhsT=wb_codes[0][:, 0, : 2 * P].bitcast(FP4X4),
-                lhsT_scale=wb_planes[0, 0][:, :P],
-                rhs=wb_codes[0][:, 0, :].bitcast(FP4X4),
-                rhs_scale=wb_planes[0, 0][:],
+                lhsT=wb_scales_raw[:].bitcast(U8)[:, 1, : 2 * P].bitcast(FP4X4),
+                lhsT_scale=wb_scales_raw[:].bitcast(U8)[:, 0, :P],
+                rhs=wb_scales_raw[:].bitcast(U8)[:, 1, :].bitcast(FP4X4),
+                rhs_scale=wb_scales_raw[:].bitcast(U8)[:, 0, :PASS],
                 start=True,
                 stop=True,
             )
+        reorder_wb(0)
+        reorder_wb_scales(0, 0, nc.vector)
+        reorder_wb_scales(0, 1, nc.gpsimd, "wb_raw_0")
         gather_words(0, halves[0], "picked")
         gather_words(0, halves[1], "picked_second")
+        banks = [new_bank(t) for t in range(PACK)]
         for cols in halves:
             part_words(0, cols)
+            for t in range(PACK):
+                product("b", 0, 0, t, cols, banks[t][:, cols])
         for part in range(2):
             round_wa(0, 0, part, on_scalar=True)
         reorder_wb_scales(1, 0, nc.gpsimd, "picked_second")
@@ -284,7 +290,7 @@ def tile_list_stroke_maxout_logits_kernel(tc, tab, offs, wa, ba, wb_words, wb_sc
         part_words(1, whole)
 
         for t in range(PACK):
-            first_piece("b", 0, 0, t, t)
+            take_out("b", 0, 0, t, banks[t])
         quantize_wa(0, 0)
         for part in range(2):
             round_wa(0, 1, part, on_scalar=False)
@@ -322,7 +328,7 @@ def tile_list_stroke_maxout_logits_kernel(tc, tab, offs, wa, ba, wb_words, wb_sc
         for t in range(1, PACK):
             first_piece("a", 1, 1, t, bank_number + 2 * t + 1, (1, 0))
         quantize_h(0, 0, whole)
-        group_h(1, 0, halves[0], on_scalar=False)
+        group_h_on_gpsimd(1, 0, halves[0])
         group_h(1, 0, halves[1], on_scalar=True)
 
         for pair in range(2):

@@ -29,7 +29,7 @@ ROWS = 32
 LIST_ROWS = 16
 BANKS = 8
 RUN = 4
-WARM_UP = 6
+WARM_UP = 3
 
 
 def tile_list_stroke_maxout_logits_kernel(tc, tab, offs, wa, ba, wb_words, wb_scales, bb, wc_words, wc_scales, bc, out):
@@ -263,19 +263,18 @@ def tile_list_stroke_maxout_logits_kernel(tc, tab, offs, wa, ba, wb_words, wb_sc
         load_wc()
 
         warm = new_bank(BANKS - 1)
-        for i in range(WARM_UP):
-            nc.tensor.matmul_mx(
-                out=warm[:],
-                lhsT=wb_scales_raw[:].bitcast(U8)[:, 1, : 2 * P].bitcast(FP4X4),
-                lhsT_scale=wb_scales_raw[:].bitcast(U8)[:, 0, :P],
-                rhs=wb_scales_raw[:].bitcast(U8)[:, 1, :].bitcast(FP4X4),
-                rhs_scale=wb_scales_raw[:].bitcast(U8)[:, 0, :PASS],
-                start=True,
-                stop=True,
-            )
+
+        def warm_up(codes, plane):
+            for i in range(WARM_UP):
+                nc.tensor.matmul_mx(
+                    out=warm[:], lhsT=codes[:, : 2 * P].bitcast(FP4X4), lhsT_scale=plane[:, :P], rhs=codes.bitcast(FP4X4), rhs_scale=plane, start=True, stop=True
+                )
+
+        warm_up(wb_scales_raw[:].bitcast(U8)[:, 1, :], wb_scales_raw[:].bitcast(U8)[:, 0, :PASS])
         reorder_wb(0)
         reorder_wb_scales(0, 0, nc.vector)
         reorder_wb_scales(0, 1, nc.gpsimd, "wb_raw_0")
+        warm_up(wb_codes[0][:, 0, :], wb_planes[0, 0][:])
         gather_words(0, halves[0], "picked")
         gather_words(0, halves[1], "picked_second")
         banks = [new_bank(t) for t in range(PACK)]

@@ -30,6 +30,7 @@ LIST_ROWS = 16
 BANKS = 8
 RUN = 4
 WARM_UP = 3
+ALIGN = 256
 
 
 def tile_list_stroke_maxout_logits_kernel(tc, tab, offs, wa, ba, wb_words, wb_scales, bb, wc_words, wc_scales, bc, out):
@@ -40,7 +41,7 @@ def tile_list_stroke_maxout_logits_kernel(tc, tab, offs, wa, ba, wb_words, wb_sc
         psum = ctx.enter_context(tc.psum_pool(name="psum", bufs=1))
 
         def held(name, shape, dtype, tag=""):
-            return keep.tile(shape, dtype, name=name, tag=tag or name, align_bytes=256)
+            return keep.tile(shape, dtype, name=name, tag=tag or name, align_bytes=ALIGN)
 
         offsets = lists.tile([P, S // LIST_ROWS], U16, name="offsets")
         tab_scales = held("tab_scales", [P, T // 4], I32)
@@ -129,11 +130,11 @@ def tile_list_stroke_maxout_logits_kernel(tc, tab, offs, wa, ba, wb_words, wb_sc
 
         wb_planes = {}
 
-        def reorder_wb_scales(g, a, engine, tag=""):
-            wb_planes[g, a] = held("wb_planes_%d_%d" % (g, a), [P, PASS], U8, tag)
-            engine.tensor_copy(
-                out=wb_planes[g, a][:].rearrange("p (t m) -> p t m", t=PACK),
-                in_=wb_scales_raw[:].bitcast(U8)[:, a, PASS * g : PASS * (g + 1)].rearrange("p (m t) -> p t m", t=PACK),
+        def reorder_wb_scales(g, tag=""):
+            wb_planes[g] = held("wb_planes_%d" % g, [P, 2, PASS], U8, tag)
+            nc.gpsimd.tensor_copy(
+                out=wb_planes[g][:].rearrange("p a (t m) -> p a t m", t=PACK),
+                in_=wb_scales_raw[:].bitcast(U8)[:, :, PASS * g : PASS * (g + 1)].rearrange("p a (m t) -> p a t m", t=PACK),
             )
 
         wa_bf16 = {key: held("wa_bf16_%d_%d" % key, [P, PACK, P, PACK], BF16) for key in pairs}
@@ -167,7 +168,7 @@ def tile_list_stroke_maxout_logits_kernel(tc, tab, offs, wa, ba, wb_words, wb_sc
                     scale = wa_planes[g, a][:, P * t : P * (t + 1)]
                 else:
                     weights = wb_codes[g][:, a, 2 * P * t : 2 * P * (t + 1)].bitcast(FP4X4)
-                    scale = wb_planes[g, a][:, P * t : P * (t + 1)]
+                    scale = wb_planes[g][:, a, P * t : P * (t + 1)]
                 nc.tensor.matmul_mx(out=sums, lhsT=weights, lhsT_scale=scale, rhs=codes, rhs_scale=plane, start=(a == passes[0]), stop=(a == passes[1]))
 
         bias_of = {"a": ba_sb, "b": bb_sb}
@@ -271,10 +272,9 @@ def tile_list_stroke_maxout_logits_kernel(tc, tab, offs, wa, ba, wb_words, wb_sc
                 )
 
         warm_up(wb_scales_raw[:].bitcast(U8)[:, 1, :], wb_scales_raw[:].bitcast(U8)[:, 0, :PASS])
+        reorder_wb_scales(0)
         reorder_wb(0)
-        reorder_wb_scales(0, 0, nc.vector)
-        reorder_wb_scales(0, 1, nc.gpsimd, "wb_raw_0")
-        warm_up(wb_codes[0][:, 0, :], wb_planes[0, 0][:])
+        warm_up(wb_codes[0][:, 0, :], wb_planes[0][:, 0, :])
         gather_words(0, halves[0], "picked")
         gather_words(0, halves[1], "picked_second")
         banks = [new_bank(t) for t in range(PACK)]
@@ -284,7 +284,7 @@ def tile_list_stroke_maxout_logits_kernel(tc, tab, offs, wa, ba, wb_words, wb_sc
                 product("b", 0, 0, t, cols, banks[t][:, cols])
         for part in range(2):
             round_wa(0, 0, part, on_scalar=True)
-        reorder_wb_scales(1, 0, nc.gpsimd, "picked_second")
+        reorder_wb_scales(1, "picked_second")
         gather_words(1, whole, "picked")
         part_words(1, whole)
 
@@ -294,7 +294,6 @@ def tile_list_stroke_maxout_logits_kernel(tc, tab, offs, wa, ba, wb_words, wb_sc
         for part in range(2):
             round_wa(0, 1, part, on_scalar=False)
         reorder_wb(1)
-        reorder_wb_scales(1, 1, nc.vector, "picked")
         quantize_wa(0, 1)
         for t in range(PACK):
             first_piece("b", 0, 1, t, PACK + t)

from contextlib import ExitStack

import concourse.mybir as mybir

K, T, S, H, N = 1024, 2048, 1024, 1024, 256
FLOPS = 2 * S * (2 * K * H + H * N)

F32 = mybir.dt.float32
BF16 = mybir.dt.bfloat16
I32 = mybir.dt.int32
U32 = mybir.dt.uint32
U16 = mybir.dt.uint16
U8 = mybir.dt.uint8
FP8X4 = mybir.dt.float8_e4m3fn_x4
FP4X4 = mybir.dt.float4_e2m1fn_x4
IDENTITY = mybir.ActivationFunctionType.Identity
ADD = mybir.AluOpType.add
MAX = mybir.AluOpType.max
MULT = mybir.AluOpType.mult

P = 128
PACK = 4
PASS = P * PACK
QUADS = 4
QROWS = 4
HALF = 512
TABLE_WORD_BYTES = 4 * P * T
ROWS = 32
LIST_ROWS = 16
BANKS = 8
RUN = 4
WARM_UP = 3
ALIGN = 256


def tile_list_stroke_maxout_logits_kernel(tc, tab, offs, wa, ba, wb_words, wb_scales, bb, wc_words, wc_scales, bc, out):
    nc = tc.nc
    with ExitStack() as ctx:
        lists = ctx.enter_context(tc.tile_pool(name="lists", bufs=1))
        keep = ctx.enter_context(tc.tile_pool(name="keep", bufs=1))
        psum = ctx.enter_context(tc.psum_pool(name="psum", bufs=1))

        def held(name, shape, dtype, tag=""):
            return keep.tile(shape, dtype, name=name, tag=tag or name, align_bytes=ALIGN)

        offsets = lists.tile([P, S // LIST_ROWS], U16, name="offsets")
        tab_scales = held("tab_scales", [P, T // 4], I32)
        tab_words = held("tab_words", [P, T], I32)
        wb_scales_raw = held("wb_scales_raw", [P, 2, H // 4], I32)
        wb_raw = [held("wb_raw_%d" % g, [P, 2, PASS // 2], I32) for g in range(2)]
        ba_sb = held("ba_sb", [P, 2, PACK], F32)
        bb_sb = held("bb_sb", [P, 2, PACK], F32)
        bc_sb = held("bc_sb", [P, 2], F32)
        v_planes = held("v_planes", [P, 2, S // 4], I32)
        wc_codes = held("wc_codes", [P, 2, N], I32)
        wc_planes = held("wc_planes", [P, N // 4], I32)
        pairs = [(i, j) for i in range(2) for j in range(2)]
        wa_raw = {(g, a, part): held("wa_raw_%d_%d_%d" % (g, a, part), [P, PACK, PASS // 2], F32) for g, a in pairs for part in range(2)}

        def load_wa(g, a, part):
            first = PASS * g + part * (PASS // 2)
            rows = wa[PASS * a : PASS * (a + 1), first : first + PASS // 2].rearrange("(p j) c -> p j c", j=PACK)
            nc.sync.dma_start(out=wa_raw[g, a, part][:], in_=rows)

        def load_wb(g):
            words = wb_words.bitcast(I32)[:, :, (PASS // 2) * g : (PASS // 2) * (g + 1)]
            nc.sync.dma_start(out=wb_raw[g][:], in_=words.rearrange("a p c -> p a c"))

        def load_bias(tile, bias):
            nc.gpsimd.dma_start(out=tile[:], in_=bias.rearrange("(g p t) -> p g t", g=2, t=PACK))

        whole = slice(0, HALF)
        halves = [slice(0, HALF // 2), slice(HALF // 2, HALF)]

        nc.vector.memset(wb_scales_raw[:], 0)
        nc.vector.memset(tab_scales[ROWS : 2 * ROWS, :], 0)
        nc.vector.memset(tab_scales[2 * ROWS :, :], 0)
        early = held("early", [P, 2], F32)
        nc.vector.memset(early[:, :1], 0.0)
        nc.scalar.activation(out=early[:, 1:], in_=early[:, :1], func=IDENTITY)
        nc.vector.memset(v_planes[:], 0)
        nc.vector.memset(wc_planes[:], 0)

        picked_scales = held("picked_scales", [P, S], U8)

        def load_head():
            nc.sync.dma_start(offsets[:], offs)
            nc.sync.dma_start(out=tab_scales[:ROWS, :], in_=tab[0, TABLE_WORD_BYTES:].rearrange("(a n c) -> n a c", a=2, n=ROWS // 2).bitcast(I32))
            load_wb(0)
            for q in range(QUADS):
                rows = wb_scales.bitcast(I32)[:, QROWS * q : QROWS * (q + 1), :]
                nc.sync.dma_start(out=wb_scales_raw[32 * q : 32 * q + QROWS, :, :], in_=rows.rearrange("a w c -> w a c"))
            nc.sync.dma_start(out=tab_words[:], in_=tab[0, :TABLE_WORD_BYTES].rearrange("(p b) -> p b", p=P).bitcast(I32))

        def gather_scales():
            nc.vector.tensor_copy(out=picked_scales[:], in_=tab_scales[:].bitcast(U8).indirect(offsets[:]))
            for q in range(QUADS):
                rows = picked_scales[2 * QROWS * q : 2 * QROWS * (q + 1), :]
                nc.sync.dma_start(out=v_planes[32 * q : 32 * q + QROWS, :, :], in_=rows.bitcast(I32))

        def load_wc():
            nc.sync.dma_start(out=wc_codes[:], in_=wc_words.rearrange("a p c i -> p a (c i)").bitcast(I32))
            for q in range(QUADS):
                nc.sync.dma_start(out=wc_planes[32 * q : 32 * q + 2 * QROWS, :], in_=wc_scales.bitcast(I32)[:, QROWS * q : QROWS * (q + 1), :])
            with nc.allow_non_contiguous_dma(reason="one bias value for each partition"):
                nc.sync.dma_start(out=bc_sb[:], in_=bc.rearrange("(c p) -> p c", p=P))

        picked = {}
        v_codes = [held("v_codes_%d" % u, [P, 2, HALF], U16) for u in range(2)]

        def gather_words(u, cols, tag):
            picked[u, cols.start] = held("picked_%d_%d" % (u, cols.start), [P, cols.stop - cols.start], U32, tag)
            entries = offsets[:, (HALF * u + cols.start) // LIST_ROWS : (HALF * u + cols.stop) // LIST_ROWS]
            nc.vector.tensor_copy(out=picked[u, cols.start][:], in_=tab_words[:].bitcast(U32).indirect(entries))

        def part_words(u, cols):
            nc.vector.tensor_copy(out=v_codes[u][:, :, cols], in_=picked[u, cols.start][:].bitcast(U16).rearrange("p (j a) -> p a j", a=2))

        def v_operand(u, a, cols):
            return v_codes[u][:, a, cols].bitcast(FP4X4), v_planes[:].bitcast(U8)[:, a, HALF * u + cols.start : HALF * u + cols.stop]

        wb_codes = {}

        def reorder_wb(g):
            wb_codes[g] = held("wb_codes_%d" % g, [P, 2, 2 * PASS], U8)
            nc.vector.tensor_copy(
                out=wb_codes[g][:].bitcast(U16).rearrange("p a (t m) -> p a t m", t=PACK),
                in_=wb_raw[g][:].bitcast(U16).rearrange("p a (m t) -> p a t m", t=PACK),
            )

        wb_planes = {}

        def reorder_wb_scales(g, tag=""):
            wb_planes[g] = held("wb_planes_%d" % g, [P, 2, PASS], U8, tag)
            nc.gpsimd.tensor_copy(
                out=wb_planes[g][:].rearrange("p a (t m) -> p a t m", t=PACK),
                in_=wb_scales_raw[:].bitcast(U8)[:, :, PASS * g : PASS * (g + 1)].rearrange("p a (m t) -> p a t m", t=PACK),
            )

        wa_bf16 = {key: held("wa_bf16_%d_%d" % key, [P, PACK, P, PACK], BF16) for key in pairs}
        wa_codes = {key: held("wa_codes_%d_%d" % key, [P, PASS], U32) for key in pairs}
        wa_planes = {key: held("wa_planes_%d_%d" % key, [P, PASS], U8) for key in pairs}

        def round_wa(g, a, part, on_scalar):
            m = slice(part * (P // 2), (part + 1) * (P // 2))
            src = wa_raw[g, a, part][:].rearrange("p j (m t) -> p m j t", t=PACK)
            dst = wa_bf16[g, a][:].rearrange("p t m j -> p m j t")[:, m]
            if on_scalar:
                nc.scalar.activation(out=dst, in_=src, func=IDENTITY)
            else:
                nc.vector.tensor_copy(out=dst, in_=src)

        def quantize_wa(g, a):
            nc.vector.quantize_mx(
                out=wa_codes[g, a][:].bitcast(FP8X4),
                scales=wa_planes[g, a][:],
                in_=wa_bf16[g, a][:].rearrange("p t m j -> p (t m j)"),
            )

        def new_bank(number):
            return psum.tile([P, HALF], F32, name="bank_%d" % (number % BANKS))

        def product(piece, g, u, t, cols, sums, passes=(0, 1)):
            for a in passes:
                codes, plane = v_operand(u, a, cols)
                if piece == "a":
                    weights = wa_codes[g, a][:, P * t : P * (t + 1)].bitcast(FP8X4)
                    scale = wa_planes[g, a][:, P * t : P * (t + 1)]
                else:
                    weights = wb_codes[g][:, a, 2 * P * t : 2 * P * (t + 1)].bitcast(FP4X4)
                    scale = wb_planes[g][:, a, P * t : P * (t + 1)]
                nc.tensor.matmul_mx(out=sums, lhsT=weights, lhsT_scale=scale, rhs=codes, rhs_scale=plane, start=(a == passes[0]), stop=(a == passes[1]))

        bias_of = {"a": ba_sb, "b": bb_sb}
        sums_buffer = {(0, 0): "wa_raw_0_0_1", (1, 0): "wa_raw_1_0_1"}
        first_sums = {key: held("first_sums_%d_%d" % key, [P, PACK, HALF], F32, sums_buffer.get(key, "")) for key in pairs}
        h_rows = {key: held("h_rows_%d_%d" % key, [P, PACK, HALF], BF16, "wa_raw_1_0_0" if key == (0, 0) else "") for key in pairs}
        h_grouped = {key: held("h_grouped_%d_%d" % key, [P, HALF, PACK], BF16, "h_grouped_0_0" if key == (1, 0) else "") for key in pairs}
        h_codes = {key: held("h_codes_%d_%d" % key, [P, HALF], U32, sums_buffer[1, 0] if key == (0, 0) else "") for key in pairs}
        h_planes = {key: held("h_planes_%d_%d" % key, [P, HALF], U8) for key in pairs}

        def take_out(piece, g, u, t, bank):
            nc.scalar.activation(out=first_sums[g, u][:, t, :], in_=bank[:], func=IDENTITY, bias=bias_of[piece][:, g, t : t + 1])

        def first_piece(piece, g, u, t, bank_number, passes=(0, 1)):
            bank = new_bank(bank_number)
            product(piece, g, u, t, whole, bank[:], passes)
            take_out(piece, g, u, t, bank)

        def maxout(piece, g, u, t, sums, cols):
            nc.vector.scalar_tensor_tensor(
                out=h_rows[g, u][:, t, cols],
                in0=sums,
                scalar=bias_of[piece][:, g, t : t + 1],
                in1=first_sums[g, u][:, t, cols],
                op0=ADD,
                op1=MAX,
            )

        def second_piece(piece, g, u, t, bank_number):
            bank = new_bank(bank_number)
            product(piece, g, u, t, whole, bank[:])
            maxout(piece, g, u, t, bank[:], whole)

        def second_piece_narrow(piece, g, u, pair, cols, bank_number):
            bank = new_bank(bank_number)
            for i in range(2):
                product(piece, g, u, 2 * pair + i, cols, bank[:, halves[i]])
            for i in range(2):
                maxout(piece, g, u, 2 * pair + i, bank[:, halves[i]], cols)

        def group_h(g, u, cols, on_scalar):
            src = h_rows[g, u][:, :, cols].rearrange("p t (c i) -> p c t i", i=RUN)
            dst = h_grouped[g, u][:, cols, :].rearrange("p (c i) t -> p c t i", i=RUN)
            if on_scalar:
                nc.scalar.copy(out=dst, in_=src)
            else:
                nc.vector.tensor_copy(out=dst, in_=src)

        def group_h_on_gpsimd(g, u, cols):
            nc.gpsimd.tensor_scalar(
                out=h_grouped[g, u][:, cols, :], in0=h_rows[g, u][:, :, cols].rearrange("p t c -> p c t"), scalar1=1.0, scalar2=0.0, op0=MULT, op1=ADD
            )

        def quantize_h(g, u, cols):
            nc.vector.quantize_mx(
                out=h_codes[g, u][:, cols].bitcast(FP8X4),
                scales=h_planes[g, u][:, cols],
                in_=h_grouped[g, u][:, cols, :].rearrange("p j t -> p (j t)"),
            )

        def logits(u, cols, both_engines, bank_number):
            width = cols.stop - cols.start
            for c in range(N // P):
                bank = new_bank(bank_number + c)
                for g in range(2):
                    nc.tensor.matmul_mx(
                        out=bank[:, :width],
                        lhsT=wc_codes[:, g, P * c : P * (c + 1)].bitcast(FP8X4),
                        lhsT_scale=wc_planes[:].bitcast(U8)[QROWS * g :, P * c : P * (c + 1)],
                        rhs=h_codes[g, u][:, cols].bitcast(FP8X4),
                        rhs_scale=h_planes[g, u][:, cols],
                        start=(g == 0),
                        stop=(g == 1),
                    )
                result = held("result_%d_%d_%d" % (u, cols.start, c), [P, width], F32)
                if both_engines and c == 1:
                    nc.vector.tensor_scalar_add(out=result[:], in0=bank[:, :width], scalar1=bc_sb[:, c : c + 1])
                else:
                    nc.scalar.activation(out=result[:], in_=bank[:, :width], func=IDENTITY, bias=bc_sb[:, c : c + 1])
                nc.sync.dma_start(out=out[P * c : P * (c + 1), HALF * u + cols.start : HALF * u + cols.stop], in_=result[:])

        load_bias(bb_sb, bb)
        load_bias(ba_sb, ba)
        load_head()
        load_wa(0, 0, 0)
        gather_scales()
        load_wa(0, 0, 1)
        for g, a in pairs[1:]:
            for part in range(2):
                load_wa(g, a, part)
            if g == 0:
                load_wb(1)
        load_wc()

        warm = new_bank(BANKS - 1)

        def warm_up(codes, plane):
            for i in range(WARM_UP):
                nc.tensor.matmul_mx(
                    out=warm[:], lhsT=codes[:, : 2 * P].bitcast(FP4X4), lhsT_scale=plane[:, :P], rhs=codes.bitcast(FP4X4), rhs_scale=plane, start=True, stop=True
                )

        warm_up(wb_scales_raw[:].bitcast(U8)[:, 1, :], wb_scales_raw[:].bitcast(U8)[:, 0, :PASS])
        reorder_wb_scales(0)
        reorder_wb(0)
        warm_up(wb_codes[0][:, 0, :], wb_planes[0][:, 0, :])
        gather_words(0, halves[0], "picked")
        gather_words(0, halves[1], "picked_second")
        banks = [new_bank(t) for t in range(PACK)]
        for cols in halves:
            part_words(0, cols)
            for t in range(PACK):
                product("b", 0, 0, t, cols, banks[t][:, cols])
        for part in range(2):
            round_wa(0, 0, part, on_scalar=True)
        reorder_wb_scales(1, "picked_second")
        gather_words(1, whole, "picked")
        part_words(1, whole)

        for t in range(PACK):
            take_out("b", 0, 0, t, banks[t])
        quantize_wa(0, 0)
        for part in range(2):
            round_wa(0, 1, part, on_scalar=False)
        reorder_wb(1)
        quantize_wa(0, 1)
        for t in range(PACK):
            first_piece("b", 0, 1, t, PACK + t)
        round_wa(1, 0, 0, on_scalar=False)
        round_wa(1, 0, 1, on_scalar=True)

        prepare = [
            lambda: quantize_wa(1, 0),
            lambda: round_wa(1, 1, 0, on_scalar=True),
            lambda: round_wa(1, 1, 1, on_scalar=False),
            lambda: quantize_wa(1, 1),
        ]
        bank_number = 0
        for step in range(2 * PACK):
            second_piece("a", 0, step // PACK, step % PACK, bank_number)
            bank_number += 1
            if 1 <= step <= PACK:
                prepare[step - 1]()
                first_piece("b", 1, 0, step - 1, bank_number)
                bank_number += 1
        for cols in halves:
            group_h(0, 0, cols, on_scalar=True)
        group_h(0, 1, halves[0], on_scalar=True)
        group_h_on_gpsimd(0, 1, halves[1])

        for t in range(PACK):
            second_piece("a", 1, 0, t, bank_number + 2 * t)
            if t == 1:
                first_piece("a", 1, 1, 0, bank_number + 1, (1, 0))
        for t in range(1, PACK):
            first_piece("a", 1, 1, t, bank_number + 2 * t + 1, (1, 0))
        quantize_h(0, 0, whole)
        group_h_on_gpsimd(1, 0, halves[0])
        group_h(1, 0, halves[1], on_scalar=True)

        for pair in range(2):
            second_piece_narrow("b", 1, 1, pair, halves[0], PACK + pair)
        quantize_h(1, 0, whole)
        group_h(1, 1, halves[0], on_scalar=True)
        for pair in range(2):
            second_piece_narrow("b", 1, 1, pair, halves[1], PACK + 2 + pair)
        logits(0, whole, False, 0)
        quantize_h(0, 1, whole)
        group_h(1, 1, halves[1], on_scalar=False)
        quantize_h(1, 1, halves[0])
        logits(1, halves[0], False, 2)
        quantize_h(1, 1, halves[1])
        logits(1, halves[1], True, PACK)
